import numpy as np
import ml_dtypes


def mxq(x, axis, fmt="e4m3"):
    dtype, down = {"e4m3": (ml_dtypes.float8_e4m3fn, 7), "e5m2": (ml_dtypes.float8_e5m2, 14)}[fmt]
    v = np.moveaxis(np.asarray(x, np.float32).astype(ml_dtypes.bfloat16).astype(np.float64), axis, -1)
    blocks = v.reshape(v.shape[:-1] + (-1, 32))
    amax = np.abs(blocks).max(-1, keepdims=True)
    byte = np.maximum(np.where(amax > 0, np.frexp(amax)[1] - 1 + 127, 0) - down, 1)
    scale = np.exp2(byte - 127.0)
    codes = (blocks / scale).astype(np.float32).astype(dtype).astype(np.float64)
    return np.moveaxis((codes * scale).reshape(v.shape), -1, axis)


WIDE = False


def mx_kscale(k):
    if not WIDE:
        return np.ones(k)
    levels = np.array([10, -10, 5, -5, 0])
    if k % 512:
        return np.exp2(np.random.permutation(np.resize(levels, k // 32))).repeat(32)
    a = np.empty((k // 512, 16))
    for p in range(k // 512):
        a[p, :8] = np.random.permutation(np.resize(levels, 8))
        for g in range(8):
            far = levels[np.abs(levels - a[p, g]) >= 10]
            a[p, g + 8] = far[np.random.randint(len(far))]
    return np.exp2(a.ravel()).repeat(32)


def f64(x):
    return np.asarray(x).astype(np.float64)


def striped(idx):
    return np.tile(idx.reshape(-1, 16).T, (8, 1)).astype(np.uint16)


def unstriped(offs):
    return offs[:16].T.reshape(-1).astype(np.int64)


E2M1 = np.array([0.0, 0.5, 1.0, 1.5, 2.0, 3.0, 4.0, 6.0, -0.0, -0.5, -1.0, -1.5, -2.0, -3.0, -4.0, -6.0])


def pack_weight(w, fmt):
    k, n = w.shape
    w = f64(np.asarray(w, np.float32).astype(ml_dtypes.bfloat16)).reshape(k // 32, 32, n)
    amax = np.abs(w).max(1)
    if fmt == "e4m3":
        byte = np.frexp(amax)[1] - 1 + 127 - 7
    else:
        mant, ex = np.frexp(amax / 6.0)
        byte = np.where(mant > 0.5, ex, ex - 1) + 127
    byte = np.clip(np.where(amax > 0, byte, 1), 1, 254)
    scaled = (w * np.exp2(127.0 - byte)[:, None, :]).reshape(k, n).astype(np.float32)
    by_word = np.ascontiguousarray(scaled.reshape(k // 512, 128, 4, n).transpose(0, 1, 3, 2))
    if fmt == "e4m3":
        words = by_word.astype(ml_dtypes.float8_e4m3fn).view(np.uint8)
    else:
        c = by_word.astype(ml_dtypes.float4_e2m1fn).view(np.uint8) & 0xF
        words = (c[..., 0::2] | (c[..., 1::2] << 4)).reshape(k // 512, 128, 2 * n)
    return np.ascontiguousarray(words), np.ascontiguousarray(byte.astype(np.uint8).reshape(k // 512, 16, n))


def unpack_weight(words, scales, fmt):
    g, _, n = scales.shape
    words = np.ascontiguousarray(words).reshape(g, 128, n, -1)
    if fmt == "e4m3":
        vals = words.view(ml_dtypes.float8_e4m3fn).astype(np.float64)
    else:
        nib = np.empty((g, 128, n, 4), np.uint8)
        nib[..., 0::2] = words & 0xF
        nib[..., 1::2] = words >> 4
        vals = E2M1[nib]
    vals = vals * np.repeat(np.exp2(scales.astype(np.float64) - 127.0), 8, axis=1)[..., None]
    return vals.transpose(0, 1, 3, 2).reshape(g * 512, n)


def gelu(v):
    return 0.5 * v * (1.0 + np.tanh(np.sqrt(2.0 / np.pi) * (v + 0.044715 * v**3)))


def striped8(idx):
    return np.concatenate([v.reshape(-1, 16).T for v in idx]).astype(np.uint16)


def unstriped8(offs):
    return np.stack([offs[16 * g:16 * g + 16].T.reshape(-1) for g in range(8)]).astype(np.int64)


def put_heads(h, wgs, idx8, t2):
    r = np.arange(h.shape[0])
    page = np.zeros((h.shape[0], t2))
    page[r[:, None], idx8[r % 512 // 64]] = wgs[r // 4 % 128] * h
    return page


K, H, N, T, S, T2 = 1536, 1024, 512, 2048, 512, 1024

def setup_inputs():
    n = np.random.standard_normal
    s = mx_kscale(K)[:, None]
    u = mx_kscale(H)[:, None]
    tab_words, tab_scales = pack_weight(n((K, T)) * s, "e4m3")
    mix_words, mix_scales = pack_weight(0.3 * n((H, H)) / np.sqrt(H) / u, "e2m1")
    wq_words, wq_scales = pack_weight(n((H, N)) / np.sqrt(H) / u, "e4m3")
    return {
        "tab_words": tab_words, "tab_scales": tab_scales,
        "offs": striped(np.random.permutation(T)[:S]),
        "x": (0.35 * n((K, H)) / np.sqrt(K) / s).astype(np.float32),
        "xs": (n((H, S)) * u).astype(np.float32),
        "mix_words": mix_words, "mix_scales": mix_scales,
        "phase": (0.15 * n(H)).astype(np.float32),
        "amp": (np.random.uniform(1.5, 3.0, H) * u[:, 0]).astype(np.float32),
        "wgs": np.repeat(np.random.uniform(0.5, 2.0, (8, S)), 16, axis=0).astype(np.float32),
        "offs2": striped8(np.stack([np.random.permutation(T2)[:S] for _ in range(8)])),
        "cap": ((0.3 + 0.7 * n((H, T2))) * u).astype(np.float32),
        "wq_words": wq_words, "wq_scales": wq_scales,
        "base": (0.5 * n(N)).astype(np.float32),
    }

def reference(tab_words, tab_scales, offs, x, xs, mix_words, mix_scales, phase, amp,
              wgs, offs2, cap, wq_words, wq_scales, base):
    v = unpack_weight(tab_words, tab_scales, "e4m3")[:, unstriped(offs)]
    mix = unpack_weight(mix_words, mix_scales, "e2m1")
    wq = unpack_weight(wq_words, wq_scales, "e4m3")
    a = mxq(f64(x), 0, "e4m3").T @ v + mix.T @ mxq(f64(xs), 0, "e4m3")
    h = f64(amp)[:, None] * np.sin(a + f64(phase)[:, None])
    page = put_heads(h, f64(wgs), unstriped8(offs2), T2)
    z = np.minimum(page, f64(cap))
    y = wq.T @ mxq(z, 0, "e4m3")
    return y + f64(base)[:, None]

@@ -1,0 +1,346 @@
+import math
+from contextlib import ExitStack
+
+import concourse.mybir as mybir
+
+K, H, N, T, S, T2 = 1536, 1024, 512, 2048, 512, 1024
+FLOPS = 2 * K * H * S + 2 * H * H * S + 2 * H * N * T2
+
+F32 = mybir.dt.float32
+BF16 = mybir.dt.bfloat16
+I32 = mybir.dt.int32
+U32 = mybir.dt.uint32
+U16 = mybir.dt.uint16
+U8 = mybir.dt.uint8
+FP8X4 = mybir.dt.float8_e4m3fn_x4
+FP4X4 = mybir.dt.float4_e2m1fn_x4
+ALU = mybir.AluOpType
+ACT = mybir.ActivationFunctionType
+
+P = 128
+PACK = 4
+KP = P * PACK
+KA = K // KP
+HB = H // KP
+NC = N // P
+CH = 256
+NCH = T2 // CH
+PAGES = 3
+TURN = 2.0 * math.pi
+
+
+def tile_list_tariff_lane_smoothing_kernel(
+    tc, tab_words, tab_scales, offs, x, xs, mix_words, mix_scales, phase, amp,
+    wgs, offs2, cap, wq_words, wq_scales, base, out,
+):
+    nc = tc.nc
+    with ExitStack() as ctx:
+        keep = ctx.enter_context(tc.tile_pool(name="keep", bufs=1))
+        ring = ctx.enter_context(tc.tile_pool(name="ring", bufs=2))
+        psum = ctx.enter_context(tc.psum_pool(name="psum", bufs=1))
+
+        offs_sb = keep.tile([P, S // 16], U16, name="offs_sb")
+        offs2_sb = keep.tile([P, S // 16], U16, name="offs2_sb")
+        tab_s = keep.tile([P, T], U8, name="tab_s", align_bytes=64)
+        mix_s_raw = keep.tile([P, HB * H], U8, name="mix_s_raw", align_bytes=64)
+        wq_s = keep.tile([P, HB * N], U8, name="wq_s", align_bytes=64)
+        pages = [keep.tile([P, T2], F32, name=f"page{n}") for n in range(PAGES)]
+        zero = keep.tile([P, 1], F32, name="zero")
+        warm = keep.tile([P, 1], F32, name="warm")
+
+        nc.vector.memset(mix_s_raw[:].bitcast(I32), 0)
+        nc.vector.memset(tab_s[:].bitcast(I32), 0)
+        nc.vector.memset(zero[:], 0.0)
+        nc.scalar.activation(out=warm[:], in_=zero[:], func=ACT.Sin)
+        nc.vector.memset(wq_s[:].bitcast(I32), 0)
+        for page in pages:
+            nc.vector.memset(page[:], 0.0)
+
+        def load_raw(rows, name):
+            raw = ring.tile([P, PACK, KP], F32, name=name, tag="raw", bufs=5)
+            nc.sync.dma_start(out=raw[:], in_=rows.rearrange("(p j) c -> p j c", j=PACK))
+            return raw
+
+        def quantize(raw, permute, name):
+            grouped = ring.tile([P, PACK * KP], BF16, name=name + "_g", tag="grouped", bufs=3, align_bytes=64)
+            if permute:
+                nc.scalar.copy(
+                    out=grouped[:].rearrange("p (t m j) -> p m j t", t=PACK, j=PACK),
+                    in_=raw[:].rearrange("p j (m t) -> p m j t", t=PACK),
+                )
+            else:
+                nc.scalar.copy(
+                    out=grouped[:].rearrange("p (m t j) -> p m j t", t=PACK, j=PACK),
+                    in_=raw[:].rearrange("p j (m t) -> p m j t", t=PACK),
+                )
+            codes = keep.tile([P, KP], U32, name=name + "_c", align_bytes=64)
+            scales = keep.tile([P, KP], U8, name=name + "_s", align_bytes=64)
+            nc.vector.quantize_mx(out=codes[:].bitcast(FP8X4), scales=scales[:], in_=grouped[:])
+            return codes, scales
+
+        phase_sb = keep.tile([P, HB, PACK], F32, name="phase_sb")
+        amp_sb = keep.tile([P, HB, PACK], F32, name="amp_sb")
+        base_sb = keep.tile([P, NC], F32, name="base_sb")
+
+        x_raw = {}
+        tab_w = []
+
+        def load_x(b, a):
+            x_raw[b, a] = load_raw(x[a * KP : (a + 1) * KP, b * KP : (b + 1) * KP], f"x_raw{b}{a}")
+
+        def load_table(a):
+            words = keep.tile([P, T], I32, name=f"tab_w{a}")
+            nc.sync.dma_start(out=words[:], in_=tab_words[a].rearrange("p t i -> p (t i)").bitcast(I32))
+            tab_w.append(words)
+
+        nc.sync.dma_start(offs_sb[:], offs)
+        nc.sync.dma_start(out=phase_sb[:], in_=phase.rearrange("(b p i) -> p b i", b=HB, i=PACK))
+        mix_w_raw = keep.tile([P, HB * H // 2], I32, name="mix_w_raw")
+        nc.sync.dma_start(
+            out=mix_w_raw[:].rearrange("p (a c) -> p a c", a=HB),
+            in_=mix_words.bitcast(I32).rearrange("a p c -> p a c"),
+        )
+        xs_raw = [load_raw(xs[0:KP, :], "xs_raw0")]
+        for q in range(4):
+            nc.sync.dma_start(
+                out=mix_s_raw[32 * q : 32 * q + 4, :].bitcast(I32).rearrange("r (a c) -> r a c", a=HB),
+                in_=mix_scales[:, 4 * q : 4 * q + 4, :].bitcast(I32).rearrange("a r c -> r a c"),
+            )
+        xs_raw.append(load_raw(xs[KP : 2 * KP, :], "xs_raw1"))
+        load_x(0, 0)
+        load_table(0)
+        for q in range(4):
+            nc.sync.dma_start(
+                out=tab_s[32 * q : 32 * q + 4 * KA, :].bitcast(I32),
+                in_=tab_scales[:, 4 * q : 4 * q + 4, :].bitcast(I32),
+            )
+        load_x(0, 1)
+        load_x(0, 2)
+        load_table(1)
+        load_table(2)
+        nc.sync.dma_start(offs2_sb[:], offs2)
+        wgs_sb = keep.tile([P, S], F32, name="wgs_sb")
+        nc.sync.dma_start(out=wgs_sb[:], in_=wgs)
+        nc.sync.dma_start(out=amp_sb[:], in_=amp.rearrange("(b p i) -> p b i", b=HB, i=PACK))
+
+        cap_sb = {}
+
+        def load_cap(b):
+            rows = cap[b * KP : (b + 1) * KP, :].rearrange("(p i) t -> p i t", i=PACK)
+            for u in range(2):
+                pair = keep.tile([P, 2, T2], F32, name=f"cap{b}{u}")
+                nc.sync.dma_start(out=pair[:], in_=rows[:, 2 * u : 2 * u + 2, :])
+                cap_sb[b, 2 * u] = pair[:, 0, :]
+                cap_sb[b, 2 * u + 1] = pair[:, 1, :]
+
+        load_cap(0)
+        for a in range(KA):
+            load_x(1, a)
+        load_cap(1)
+        wq_w = keep.tile([P, HB * N], I32, name="wq_w", align_bytes=64)
+        nc.sync.dma_start(
+            out=wq_w[:].rearrange("p (a c) -> p a c", a=HB),
+            in_=wq_words.rearrange("a p c i -> p a (c i)").bitcast(I32),
+        )
+        for q in range(4):
+            nc.sync.dma_start(
+                out=wq_s[32 * q : 32 * q + 4, :].bitcast(I32).rearrange("r (a c) -> r a c", a=HB),
+                in_=wq_scales[:, 4 * q : 4 * q + 4, :].bitcast(I32).rearrange("a r c -> r a c"),
+            )
+
+        with nc.allow_non_contiguous_dma(reason="one bias value to a partition"):
+            nc.sync.dma_start(out=base_sb[:], in_=base.rearrange("(c p) -> p c", p=P))
+
+        shift = keep.tile([P, HB * PACK], F32, name="shift")
+        nc.vector.tensor_scalar(
+            out=shift[:], in0=phase_sb[:].rearrange("p b i -> p (b i)"),
+            scalar1=1.0 / TURN, scalar2=-0.25, op0=ALU.mult, op1=ALU.add,
+        )
+        mix_w = keep.tile([P, HB * H * 2], U8, name="mix_w", align_bytes=64)
+        nc.vector.tensor_copy(
+            out=mix_w[:].bitcast(U16).rearrange("p (g t m) -> p g t m", t=PACK, m=P),
+            in_=mix_w_raw[:].bitcast(U16).rearrange("p (g m t) -> p g t m", t=PACK, m=P),
+        )
+        mix_s = keep.tile([P, HB * H], U8, name="mix_s", align_bytes=64)
+        nc.vector.tensor_copy(
+            out=mix_s[:].rearrange("p (g t m) -> p g t m", t=PACK, m=P),
+            in_=mix_s_raw[:].rearrange("p (g m t) -> p g t m", t=PACK, m=P),
+        )
+        xs_q = [quantize(xs_raw[a], False, f"xs{a}") for a in range(HB)]
+        x_q = {}
+        v_w = []
+
+        def gather_words(a):
+            picked = keep.tile([P, S], U32, name=f"v_w{a}", align_bytes=64)
+            nc.vector.tensor_copy(picked[:], tab_w[a][:].bitcast(U32).indirect(offs_sb[:]))
+            v_w.append(picked)
+
+        x_q[0, 0] = quantize(x_raw[0, 0], True, "x00")
+        gather_words(0)
+        v_s = keep.tile([P, S], U8, name="v_s", align_bytes=64)
+        nc.vector.tensor_copy(v_s[:], tab_s[:].indirect(offs_sb[:]))
+        for a in range(1, KA):
+            x_q[0, a] = quantize(x_raw[0, a], True, f"x0{a}")
+        for a in range(1, KA):
+            gather_words(a)
+
+        accs = [psum.tile([P, S], F32, name=f"acc{n}", tag=f"bank{n}") for n in range(HB * PACK)]
+
+        def mix_passes(b):
+            for a in range(HB):
+                for i in range(PACK):
+                    col = a * H + b * KP + i * P
+                    nc.tensor.matmul_mx(
+                        out=accs[PACK * b + i][:],
+                        lhsT=mix_w[:, 2 * col : 2 * (col + P)].bitcast(FP4X4),
+                        lhsT_scale=mix_s[:, col : col + P],
+                        rhs=xs_q[a][0][:].bitcast(FP8X4), rhs_scale=xs_q[a][1][:],
+                        start=(a == 0), stop=False,
+                    )
+
+        def table_passes(b):
+            for a in range(KA):
+                codes, scales = x_q[b, a]
+                for i in range(PACK):
+                    nc.tensor.matmul_mx(
+                        out=accs[PACK * b + i][:],
+                        lhsT=codes[:, i * P : (i + 1) * P].bitcast(FP8X4),
+                        lhsT_scale=scales[:, i * P : (i + 1) * P],
+                        rhs=v_w[a][:].bitcast(FP8X4), rhs_scale=v_s[4 * a : P, :],
+                        start=False, stop=(a == KA - 1),
+                    )
+
+        def sine(acc, n):
+            w = ring.tile([P, S], F32, name=f"w{n}", tag="w", bufs=4)
+            nc.scalar.activation(out=w[:], in_=acc[:], func=ACT.Abs, bias=shift[:, n : n + 1], scale=1.0 / TURN)
+            k = ring.tile([P, S], U32, name=f"k{n}", tag="k", bufs=3)
+            nc.scalar.activation(out=k[:], in_=w[:], func=ACT.Copy, bias=-0.25, scale=1.0)
+            m = ring.tile([P, S], F32, name=f"m{n}", tag="m", bufs=2)
+            nc.vector.scalar_tensor_tensor(
+                out=m[:], in0=k[:].bitcast(I32), scalar=0.25, in1=w[:], op0=ALU.add, op1=ALU.subtract,
+            )
+            s = ring.tile([P, S], F32, name=f"s{n}", tag="s", bufs=3)
+            nc.scalar.activation(out=s[:], in_=m[:], func=ACT.Sin, scale=TURN)
+            return s
+
+        def scatter(s, n):
+            nc.vector.tensor_tensor(pages[n % PAGES][:].indirect(offs2_sb[:]), s[:], wgs_sb[:], ALU.mult)
+
+        z_rows = [keep.tile([P, PACK * T2], BF16, name=f"z_rows{b}") for b in range(HB)]
+
+        def capped(n, c0, c1):
+            b, i = divmod(n, PACK)
+            nc.vector.scalar_tensor_tensor(
+                out=z_rows[b][:, i * T2 + c0 : i * T2 + c1], in0=pages[n % PAGES][:, c0:c1],
+                scalar=amp_sb[:, b, i : i + 1], in1=cap_sb[b, i][:, c0:c1], op0=ALU.mult, op1=ALU.min,
+            )
+
+        z_c = [keep.tile([P, T2], U32, name=f"z_c{b}", align_bytes=64) for b in range(HB)]
+        z_s = [keep.tile([P, T2], U8, name=f"z_s{b}", align_bytes=64) for b in range(HB)]
+
+        def weave(b, q, copy):
+            woven = ring.tile([P, CH * PACK], BF16, name=f"woven{b}{q}", tag="woven", bufs=4, align_bytes=64)
+            copy(
+                out=woven[:].rearrange("p (m t i) -> p m i t", t=PACK, i=PACK),
+                in_=z_rows[b][:].rearrange("p (i c) -> p i c", i=PACK)[:, :, q * CH : (q + 1) * CH].rearrange(
+                    "p i (m t) -> p m i t", t=PACK
+                ),
+            )
+            return woven
+
+        def quantize_z(b, q, woven):
+            cols = slice(q * CH, (q + 1) * CH)
+            nc.vector.quantize_mx(out=z_c[b][:, cols].bitcast(FP8X4), scales=z_s[b][:, cols], in_=woven[:])
+
+        def second_pass(b, q, banks):
+            cols = slice(q * CH, (q + 1) * CH)
+            for h in range(2):
+                for e in range(2):
+                    col = b * N + (2 * h + e) * P
+                    nc.tensor.matmul_mx(
+                        out=banks[h][:, e * CH : (e + 1) * CH],
+                        lhsT=wq_w[:, col : col + P].bitcast(FP8X4), lhsT_scale=wq_s[:, col : col + P],
+                        rhs=z_c[b][:, cols].bitcast(FP8X4), rhs_scale=z_s[b][:, cols],
+                        start=(b == 0 and e == 0), stop=(b == HB - 1 and e == 1),
+                    )
+
+        mix_passes(0)
+        table_passes(0)
+        mix_passes(1)
+        sines = {0: sine(accs[0], 0), 1: sine(accs[1], 1)}
+        clock = keep.tile([P, 2], F32, name="clock")
+        nc.gpsimd.tensor_copy(clock[:, 0:1], sines[0][:, 0:1])
+        scatter(sines[0], 0)
+        sines[2] = sine(accs[2], 2)
+        scatter(sines[1], 1)
+        capped(0, 0, T2)
+        sines[3] = sine(accs[3], 3)
+        for a in range(KA):
+            x_q[1, a] = quantize(x_raw[1, a], True, f"x1{a}")
+        table_passes(1)
+        scatter(sines[2], 2)
+        capped(1, 0, T2)
+        sines[4] = sine(accs[4], 4)
+        scatter(sines[3], 3)
+        capped(2, 0, T2)
+        sines[5] = sine(accs[5], 5)
+        scatter(sines[4], 4)
+        capped(3, 0, T2)
+        sines[6] = sine(accs[6], 6)
+        sines[7] = sine(accs[7], 7)
+        scatter(sines[5], 5)
+        capped(4, 0, T2)
+        banks = [
+            [psum.tile([P, 2 * CH], F32, name=f"y{q}{h}", tag=f"bank{2 * q + h}") for h in range(2)]
+            for q in range(NCH)
+        ]
+        woven0 = [weave(0, q, nc.scalar.copy) for q in range(NCH)]
+        scatter(sines[6], 6)
+        capped(5, 0, T2)
+        for q in range(NCH):
+            quantize_z(0, q, woven0[q])
+            second_pass(0, q, banks[q])
+        scatter(sines[7], 7)
+        nc.gpsimd.tensor_copy(clock[:, 1:2], pages[7 % PAGES][:, 0:1])
+        capped(6, 0, T2)
+        def emit(q):
+            for h in range(2):
+                staged = ring.tile([P, 2 * CH], F32, name=f"staged{q}{h}", tag="staged", bufs=4)
+                if q >= NCH - 2 and h == 0:
+                    nc.vector.tensor_tensor(
+                        staged[:].rearrange("p (e t) -> p e t", e=2),
+                        banks[q][h][:].rearrange("p (e t) -> p e t", e=2),
+                        base_sb[:, 2 * h : 2 * h + 2].unsqueeze(2).to_broadcast([P, 2, CH]),
+                        ALU.add,
+                    )
+                else:
+                    for e in range(2):
+                        c = 2 * h + e
+                        nc.scalar.activation(
+                            out=staged[:, e * CH : (e + 1) * CH], in_=banks[q][h][:, e * CH : (e + 1) * CH],
+                            func=ACT.Identity, bias=base_sb[:, c : c + 1], scale=1.0,
+                        )
+                nc.sync.dma_start(
+                    out=out[2 * h * P : (2 * h + 2) * P, q * CH : (q + 1) * CH].rearrange("(e p) t -> p e t", p=P),
+                    in_=staged[:].rearrange("p (e t) -> p e t", e=2),
+                )
+
+        capped(7, 0, CH)
+        capped(7, CH, 2 * CH)
+        woven1 = {1: weave(1, 1, nc.scalar.copy)}
+        woven1[0] = weave(1, 0, nc.vector.tensor_copy)
+        capped(7, 2 * CH, 3 * CH)
+        quantize_z(1, 0, woven1[0])
+        second_pass(1, 0, banks[0])
+        emit(0)
+        capped(7, 3 * CH, 4 * CH)
+        quantize_z(1, 1, woven1[1])
+        second_pass(1, 1, banks[1])
+        emit(1)
+        woven1[2] = weave(1, 2, nc.vector.tensor_copy)
+        woven1[3] = weave(1, 3, nc.vector.tensor_copy)
+        for q in range(2, NCH):
+            quantize_z(1, q, woven1[q])
+            second_pass(1, q, banks[q])
+        for q in range(2, NCH):
+            emit(q)

@@ -26,6 +26,7 @@ NC = N // P
 CH = 256
 NCH = T2 // CH
 PAGES = 3
+HALF = S // 2
 TURN = 2.0 * math.pi
 
 
@@ -61,18 +62,13 @@ def tile_list_tariff_lane_smoothing_kernel(
             nc.sync.dma_start(out=raw[:], in_=rows.rearrange("(p j) c -> p j c", j=PACK))
             return raw
 
-        def quantize(raw, permute, name):
-            grouped = ring.tile([P, PACK * KP], BF16, name=name + "_g", tag="grouped", bufs=3, align_bytes=64)
-            if permute:
-                nc.scalar.copy(
-                    out=grouped[:].rearrange("p (t m j) -> p m j t", t=PACK, j=PACK),
-                    in_=raw[:].rearrange("p j (m t) -> p m j t", t=PACK),
-                )
-            else:
-                nc.scalar.copy(
-                    out=grouped[:].rearrange("p (m t j) -> p m j t", t=PACK, j=PACK),
-                    in_=raw[:].rearrange("p j (m t) -> p m j t", t=PACK),
-                )
+        def quantize(raw, order, copies, name, tag="grouped", bufs=4):
+            grouped = ring.tile([P, PACK * KP], BF16, name=name + "_g", tag=tag, bufs=bufs, align_bytes=64)
+            dst = grouped[:].rearrange(order + " -> p m j t", t=PACK, j=PACK)
+            src = raw[:].rearrange("p j (m t) -> p m j t", t=PACK)
+            share = P // len(copies)
+            for u, copy in enumerate(copies):
+                copy(out=dst[:, u * share : (u + 1) * share], in_=src[:, u * share : (u + 1) * share])
             codes = keep.tile([P, KP], U32, name=name + "_c", align_bytes=64)
             scales = keep.tile([P, KP], U8, name=name + "_s", align_bytes=64)
             nc.vector.quantize_mx(out=codes[:].bitcast(FP8X4), scales=scales[:], in_=grouped[:])
@@ -115,8 +111,8 @@ def tile_list_tariff_lane_smoothing_kernel(
                 in_=tab_scales[:, 4 * q : 4 * q + 4, :].bitcast(I32),
             )
         load_x(0, 1)
-        load_x(0, 2)
         load_table(1)
+        load_x(0, 2)
         load_table(2)
         nc.sync.dma_start(offs2_sb[:], offs2)
         wgs_sb = keep.tile([P, S], F32, name="wgs_sb")
@@ -125,18 +121,19 @@ def tile_list_tariff_lane_smoothing_kernel(
 
         cap_sb = {}
 
-        def load_cap(b):
+        def load_cap(b, u):
             rows = cap[b * KP : (b + 1) * KP, :].rearrange("(p i) t -> p i t", i=PACK)
-            for u in range(2):
-                pair = keep.tile([P, 2, T2], F32, name=f"cap{b}{u}")
-                nc.sync.dma_start(out=pair[:], in_=rows[:, 2 * u : 2 * u + 2, :])
-                cap_sb[b, 2 * u] = pair[:, 0, :]
-                cap_sb[b, 2 * u + 1] = pair[:, 1, :]
+            pair = keep.tile([P, 2, T2], F32, name=f"cap{b}{u}")
+            nc.sync.dma_start(out=pair[:], in_=rows[:, 2 * u : 2 * u + 2, :])
+            cap_sb[b, 2 * u] = pair[:, 0, :]
+            cap_sb[b, 2 * u + 1] = pair[:, 1, :]
 
-        load_cap(0)
+        load_cap(0, 0)
         for a in range(KA):
             load_x(1, a)
-        load_cap(1)
+        load_cap(0, 1)
+        for u in range(2):
+            load_cap(1, u)
         wq_w = keep.tile([P, HB * N], I32, name="wq_w", align_bytes=64)
         nc.sync.dma_start(
             out=wq_w[:].rearrange("p (a c) -> p a c", a=HB),
@@ -166,65 +163,96 @@ def tile_list_tariff_lane_smoothing_kernel(
             out=mix_s[:].rearrange("p (g t m) -> p g t m", t=PACK, m=P),
             in_=mix_s_raw[:].rearrange("p (g m t) -> p g t m", t=PACK, m=P),
         )
-        xs_q = [quantize(xs_raw[a], False, f"xs{a}") for a in range(HB)]
+        xs_q = [quantize(xs_raw[a], "p (m t j)", [nc.vector.tensor_copy], f"xs{a}") for a in range(HB)]
         x_q = {}
-        v_w = []
 
-        def gather_words(a):
-            picked = keep.tile([P, S], U32, name=f"v_w{a}", align_bytes=64)
-            nc.vector.tensor_copy(picked[:], tab_w[a][:].bitcast(U32).indirect(offs_sb[:]))
-            v_w.append(picked)
+        v_w = [keep.tile([P, S], U32, name=f"v_w{a}", align_bytes=64) for a in range(KA)]
 
-        x_q[0, 0] = quantize(x_raw[0, 0], True, "x00")
-        gather_words(0)
+        def gather_words(a, c0, c1):
+            nc.vector.tensor_copy(
+                v_w[a][:, c0:c1], tab_w[a][:].bitcast(U32).indirect(offs_sb[:, c0 // 16 : c1 // 16])
+            )
+
+        x_q[0, 0] = quantize(x_raw[0, 0], "p (t m j)", [nc.scalar.copy], "x00")
+        gather_words(0, 0, S)
         v_s = keep.tile([P, S], U8, name="v_s", align_bytes=64)
         nc.vector.tensor_copy(v_s[:], tab_s[:].indirect(offs_sb[:]))
-        for a in range(1, KA):
-            x_q[0, a] = quantize(x_raw[0, a], True, f"x0{a}")
-        for a in range(1, KA):
-            gather_words(a)
+        x_q[0, 1] = quantize(x_raw[0, 1], "p (t m j)", [nc.scalar.copy], "x01")
+        gather_words(1, 0, S)
+        x_q[0, 2] = quantize(x_raw[0, 2], "p (t m j)", [nc.scalar.copy, nc.vector.tensor_copy], "x02")
+        gather_words(2, 0, HALF)
+        gather_words(2, HALF, S)
 
-        accs = [psum.tile([P, S], F32, name=f"acc{n}", tag=f"bank{n}") for n in range(HB * PACK)]
+        def mix_pass(acc, n, a, c0, c1, start):
+            b, i = divmod(n, PACK)
+            col = a * H + b * KP + i * P
+            step = S if c1 - c0 == S else P
+            for c in range(c0, c1, step):
+                nc.tensor.matmul_mx(
+                    out=acc[:, c - c0 : c - c0 + step],
+                    lhsT=mix_w[:, 2 * col : 2 * (col + P)].bitcast(FP4X4),
+                    lhsT_scale=mix_s[:, col : col + P],
+                    rhs=xs_q[a][0][:, c : c + step].bitcast(FP8X4), rhs_scale=xs_q[a][1][:, c : c + step],
+                    start=(start and c == c0), stop=False,
+                )
 
-        def mix_passes(b):
+        def table_pass(acc, n, a, c0, c1):
+            b, i = divmod(n, PACK)
+            codes, scales = x_q[b, a]
+            nc.tensor.matmul_mx(
+                out=acc[:],
+                lhsT=codes[:, i * P : (i + 1) * P].bitcast(FP8X4),
+                lhsT_scale=scales[:, i * P : (i + 1) * P],
+                rhs=v_w[a][:, c0:c1].bitcast(FP8X4), rhs_scale=v_s[4 * a : P, c0:c1],
+                start=False, stop=(a == KA - 1),
+            )
+
+        def first_product(parts, first_bank):
+            accs = [
+                psum.tile([P, c1 - c0], F32, name=f"acc{n}_{c0}", tag=f"bank{(first_bank + u) % 8}")
+                for u, (n, c0, c1) in enumerate(parts)
+            ]
             for a in range(HB):
-                for i in range(PACK):
-                    col = a * H + b * KP + i * P
-                    nc.tensor.matmul_mx(
-                        out=accs[PACK * b + i][:],
-                        lhsT=mix_w[:, 2 * col : 2 * (col + P)].bitcast(FP4X4),
-                        lhsT_scale=mix_s[:, col : col + P],
-                        rhs=xs_q[a][0][:].bitcast(FP8X4), rhs_scale=xs_q[a][1][:],
-                        start=(a == 0), stop=False,
-                    )
+                for acc, (n, c0, c1) in zip(accs, parts):
+                    mix_pass(acc, n, a, c0, c1, a == 0)
+            return accs
 
-        def table_passes(b):
+        def finish_product(accs, parts):
             for a in range(KA):
-                codes, scales = x_q[b, a]
-                for i in range(PACK):
-                    nc.tensor.matmul_mx(
-                        out=accs[PACK * b + i][:],
-                        lhsT=codes[:, i * P : (i + 1) * P].bitcast(FP8X4),
-                        lhsT_scale=scales[:, i * P : (i + 1) * P],
-                        rhs=v_w[a][:].bitcast(FP8X4), rhs_scale=v_s[4 * a : P, :],
-                        start=False, stop=(a == KA - 1),
-                    )
+                for acc, (n, c0, c1) in zip(accs, parts):
+                    table_pass(acc, n, a, c0, c1)
 
-        def sine(acc, n):
-            w = ring.tile([P, S], F32, name=f"w{n}", tag="w", bufs=4)
+        def sine_tile(n, width, name):
+            if n == 3:
+                return ring.tile([P, width], F32, name=name, tag="held", bufs=1, align_bytes=64)
+            return ring.tile([P, width], F32, name=name, tag="s", bufs=3)
+
+        def fold(acc, n, c0, c1):
+            w = ring.tile([P, c1 - c0], F32, name=f"w{n}_{c0}", tag="w", bufs=4)
             nc.scalar.activation(out=w[:], in_=acc[:], func=ACT.Abs, bias=shift[:, n : n + 1], scale=1.0 / TURN)
-            k = ring.tile([P, S], U32, name=f"k{n}", tag="k", bufs=3)
-            nc.scalar.activation(out=k[:], in_=w[:], func=ACT.Copy, bias=-0.25, scale=1.0)
-            m = ring.tile([P, S], F32, name=f"m{n}", tag="m", bufs=2)
+            k = ring.tile([P, c1 - c0], U32, name=f"k{n}_{c0}", tag="k", bufs=3)
+            if n == 0:
+                nc.vector.tensor_scalar(
+                    out=k[:].bitcast(I32), in0=w[:], scalar1=-0.25, scalar2=None, op0=ALU.add
+                )
+            else:
+                nc.scalar.activation(out=k[:], in_=w[:], func=ACT.Copy, bias=-0.25, scale=1.0)
+            return w, k
+
+        def sine(acc, n, c0=0, c1=S):
+            w, k = fold(acc, n, c0, c1)
+            m = ring.tile([P, c1 - c0], F32, name=f"m{n}_{c0}", tag="m", bufs=2)
             nc.vector.scalar_tensor_tensor(
                 out=m[:], in0=k[:].bitcast(I32), scalar=0.25, in1=w[:], op0=ALU.add, op1=ALU.subtract,
             )
-            s = ring.tile([P, S], F32, name=f"s{n}", tag="s", bufs=3)
+            s = sine_tile(n, c1 - c0, f"s{n}_{c0}")
             nc.scalar.activation(out=s[:], in_=m[:], func=ACT.Sin, scale=TURN)
             return s
 
-        def scatter(s, n):
-            nc.vector.tensor_tensor(pages[n % PAGES][:].indirect(offs2_sb[:]), s[:], wgs_sb[:], ALU.mult)
+        def scatter(s, n, c0=0, c1=S):
+            nc.vector.tensor_tensor(
+                pages[n % PAGES][:].indirect(offs2_sb[:, c0 // 16 : c1 // 16]), s[:], wgs_sb[:, c0:c1], ALU.mult
+            )
 
         z_rows = [keep.tile([P, PACK * T2], BF16, name=f"z_rows{b}") for b in range(HB)]
 
@@ -238,77 +266,90 @@ def tile_list_tariff_lane_smoothing_kernel(
         z_c = [keep.tile([P, T2], U32, name=f"z_c{b}", align_bytes=64) for b in range(HB)]
         z_s = [keep.tile([P, T2], U8, name=f"z_s{b}", align_bytes=64) for b in range(HB)]
 
-        def weave(b, q, copy):
-            woven = ring.tile([P, CH * PACK], BF16, name=f"woven{b}{q}", tag="woven", bufs=4, align_bytes=64)
+        def weave(b, c0, c1, copy):
+            woven = ring.tile([P, (c1 - c0) * PACK], BF16, name=f"woven{b}_{c0}", tag="grouped", bufs=4, align_bytes=64)
             copy(
                 out=woven[:].rearrange("p (m t i) -> p m i t", t=PACK, i=PACK),
-                in_=z_rows[b][:].rearrange("p (i c) -> p i c", i=PACK)[:, :, q * CH : (q + 1) * CH].rearrange(
+                in_=z_rows[b][:].rearrange("p (i c) -> p i c", i=PACK)[:, :, c0:c1].rearrange(
                     "p i (m t) -> p m i t", t=PACK
                 ),
             )
             return woven
 
-        def quantize_z(b, q, woven):
-            cols = slice(q * CH, (q + 1) * CH)
-            nc.vector.quantize_mx(out=z_c[b][:, cols].bitcast(FP8X4), scales=z_s[b][:, cols], in_=woven[:])
+        def quantize_z(b, c0, c1, woven):
+            nc.vector.quantize_mx(out=z_c[b][:, c0:c1].bitcast(FP8X4), scales=z_s[b][:, c0:c1], in_=woven[:])
 
-        def second_pass(b, q, banks):
+        def second_pass(b, q):
             cols = slice(q * CH, (q + 1) * CH)
             for h in range(2):
                 for e in range(2):
                     col = b * N + (2 * h + e) * P
                     nc.tensor.matmul_mx(
-                        out=banks[h][:, e * CH : (e + 1) * CH],
+                        out=banks[q][h][:, e * CH : (e + 1) * CH],
                         lhsT=wq_w[:, col : col + P].bitcast(FP8X4), lhsT_scale=wq_s[:, col : col + P],
                         rhs=z_c[b][:, cols].bitcast(FP8X4), rhs_scale=z_s[b][:, cols],
                         start=(b == 0 and e == 0), stop=(b == HB - 1 and e == 1),
                     )
 
-        mix_passes(0)
-        table_passes(0)
-        mix_passes(1)
-        sines = {0: sine(accs[0], 0), 1: sine(accs[1], 1)}
-        clock = keep.tile([P, 2], F32, name="clock")
-        nc.gpsimd.tensor_copy(clock[:, 0:1], sines[0][:, 0:1])
-        scatter(sines[0], 0)
-        sines[2] = sine(accs[2], 2)
+        late = sine
+        parts0 = [(0, 0, HALF), (0, HALF, S), (1, 0, S), (2, 0, S), (3, 0, S)]
+        parts1 = [(n, 0, S) for n in range(PACK, 2 * PACK)]
+        accs0 = first_product(parts0, 7)
+        for acc, part in zip(accs0, parts0):
+            table_pass(acc, part[0], 0, part[1], part[2])
+        for lo, hi in ((0, 2), (2, 5)):
+            for a in range(1, KA):
+                for acc, part in zip(accs0[lo:hi], parts0[lo:hi]):
+                    table_pass(acc, part[0], a, part[1], part[2])
+        first_a = sine(accs0[0], 0, 0, HALF)
+        first_b = sine(accs0[1], 0, HALF, S)
+        scatter(first_a, 0, 0, HALF)
+        sines = {1: sine(accs0[2], 1)}
+        scatter(first_b, 0, HALF, S)
+        sines[2] = sine(accs0[3], 2)
+        accs1 = first_product(parts1, 4)
         scatter(sines[1], 1)
         capped(0, 0, T2)
-        sines[3] = sine(accs[3], 3)
-        for a in range(KA):
-            x_q[1, a] = quantize(x_raw[1, a], True, f"x1{a}")
-        table_passes(1)
+        for a in range(KA - 1):
+            x_q[1, a] = quantize(x_raw[1, a], "p (t m j)", [nc.scalar.copy], f"x1{a}")
+        x_q[1, 2] = quantize(x_raw[1, 2], "p (t m j)", [nc.scalar.copy], "x12", "held", 1)
+        finish_product(accs1, parts1)
+        sines[3] = late(accs0[4], 3)
         scatter(sines[2], 2)
         capped(1, 0, T2)
-        sines[4] = sine(accs[4], 4)
+        sines[4] = sine(accs1[0], 4)
         scatter(sines[3], 3)
         capped(2, 0, T2)
-        sines[5] = sine(accs[5], 5)
+        sines[5] = late(accs1[1], 5)
         scatter(sines[4], 4)
         capped(3, 0, T2)
-        sines[6] = sine(accs[6], 6)
-        sines[7] = sine(accs[7], 7)
+        sines[6] = late(accs1[2], 6)
         scatter(sines[5], 5)
         capped(4, 0, T2)
+        sines[7] = late(accs1[3], 7)
         banks = [
-            [psum.tile([P, 2 * CH], F32, name=f"y{q}{h}", tag=f"bank{2 * q + h}") for h in range(2)]
+            [psum.tile([P, 2 * CH], F32, name=f"y{q}{h}", tag=f"bank{(4 + 2 * q + h) % 8}") for h in range(2)]
             for q in range(NCH)
         ]
-        woven0 = [weave(0, q, nc.scalar.copy) for q in range(NCH)]
+        woven0 = [weave(0, u * 2 * CH, (u + 1) * 2 * CH, nc.scalar.copy) for u in range(2)]
         scatter(sines[6], 6)
         capped(5, 0, T2)
+        for u in range(2):
+            quantize_z(0, u * 2 * CH, (u + 1) * 2 * CH, woven0[u])
         for q in range(NCH):
-            quantize_z(0, q, woven0[q])
-            second_pass(0, q, banks[q])
-        scatter(sines[7], 7)
-        nc.gpsimd.tensor_copy(clock[:, 1:2], pages[7 % PAGES][:, 0:1])
+            second_pass(0, q)
         capped(6, 0, T2)
+        scatter(sines[7], 7)
+
+        stage = [ring.tile([P, 8 * CH], F32, name=f"stage{u}", tag="raw", bufs=5) for u in range(2)]
+
         def emit(q):
             for h in range(2):
-                staged = ring.tile([P, 2 * CH], F32, name=f"staged{q}{h}", tag="staged", bufs=4)
+                at = (2 * (q % 2) + h) * 2 * CH
+                staged = stage[q // 2][:, at : at + 2 * CH]
                 if q >= NCH - 2 and h == 0:
                     nc.vector.tensor_tensor(
-                        staged[:].rearrange("p (e t) -> p e t", e=2),
+                        staged.rearrange("p (e t) -> p e t", e=2),
                         banks[q][h][:].rearrange("p (e t) -> p e t", e=2),
                         base_sb[:, 2 * h : 2 * h + 2].unsqueeze(2).to_broadcast([P, 2, CH]),
                         ALU.add,
@@ -322,25 +363,28 @@ def tile_list_tariff_lane_smoothing_kernel(
                         )
                 nc.sync.dma_start(
                     out=out[2 * h * P : (2 * h + 2) * P, q * CH : (q + 1) * CH].rearrange("(e p) t -> p e t", p=P),
-                    in_=staged[:].rearrange("p (e t) -> p e t", e=2),
+                    in_=staged.rearrange("p (e t) -> p e t", e=2),
                 )
 
-        capped(7, 0, CH)
-        capped(7, CH, 2 * CH)
-        woven1 = {1: weave(1, 1, nc.scalar.copy)}
-        woven1[0] = weave(1, 0, nc.vector.tensor_copy)
-        capped(7, 2 * CH, 3 * CH)
-        quantize_z(1, 0, woven1[0])
-        second_pass(1, 0, banks[0])
+        def chunk(q):
+            return q * CH, (q + 1) * CH
+
+        capped(7, *chunk(0))
+        capped(7, *chunk(1))
+        woven1 = {1: weave(1, *chunk(1), nc.scalar.copy)}
+        woven1[0] = weave(1, *chunk(0), nc.vector.tensor_copy)
+        capped(7, *chunk(2))
+        quantize_z(1, *chunk(0), woven1[0])
+        second_pass(1, 0)
         emit(0)
-        capped(7, 3 * CH, 4 * CH)
-        quantize_z(1, 1, woven1[1])
-        second_pass(1, 1, banks[1])
+        capped(7, *chunk(3))
+        quantize_z(1, *chunk(1), woven1[1])
+        second_pass(1, 1)
         emit(1)
-        woven1[2] = weave(1, 2, nc.vector.tensor_copy)
-        woven1[3] = weave(1, 3, nc.vector.tensor_copy)
+        woven1[2] = weave(1, *chunk(2), nc.vector.tensor_copy)
+        woven1[3] = weave(1, *chunk(3), nc.vector.tensor_copy)
         for q in range(2, NCH):
-            quantize_z(1, q, woven1[q])
-            second_pass(1, q, banks[q])
+            quantize_z(1, *chunk(q), woven1[q])
+            second_pass(1, q)
         for q in range(2, NCH):
             emit(q)

@@ -20,13 +20,20 @@ ACT = mybir.ActivationFunctionType
 P = 128
 PACK = 4
 KP = P * PACK
-KA = K // KP
-HB = H // KP
-NC = N // P
-CH = 256
-NCH = T2 // CH
-PAGES = 3
+K_PASSES = K // KP
+H_PASSES = H // KP
+SLICES = H_PASSES * PACK
+LAST = SLICES - 1
+GROUP = 16
+QUADRANT = 32
+BANKS = 8
 HALF = S // 2
+CHUNK = 256
+CHUNKS = T2 // CHUNK
+VECTOR_CHUNKS = 2
+PAGES = 3
+RAW_BUFS = 5
+HELD_SLICE = 3
 TURN = 2.0 * math.pi
 
 
@@ -40,351 +47,327 @@ def tile_list_tariff_lane_smoothing_kernel(
         ring = ctx.enter_context(tc.tile_pool(name="ring", bufs=2))
         psum = ctx.enter_context(tc.psum_pool(name="psum", bufs=1))
 
-        offs_sb = keep.tile([P, S // 16], U16, name="offs_sb")
-        offs2_sb = keep.tile([P, S // 16], U16, name="offs2_sb")
+        offs_sb = keep.tile([P, S // GROUP], U16, name="offs_sb")
+        offs2_sb = keep.tile([P, S // GROUP], U16, name="offs2_sb")
         tab_s = keep.tile([P, T], U8, name="tab_s", align_bytes=64)
-        mix_s_raw = keep.tile([P, HB * H], U8, name="mix_s_raw", align_bytes=64)
-        wq_s = keep.tile([P, HB * N], U8, name="wq_s", align_bytes=64)
-        pages = [keep.tile([P, T2], F32, name=f"page{n}") for n in range(PAGES)]
+        mix_s_raw = keep.tile([P, H_PASSES * H], U8, name="mix_s_raw", align_bytes=64)
+        wq_s = keep.tile([P, H_PASSES * N], U8, name="wq_s", align_bytes=64)
+        pages = [keep.tile([P, T2], F32, name=f"page{u}") for u in range(PAGES)]
         zero = keep.tile([P, 1], F32, name="zero")
-        warm = keep.tile([P, 1], F32, name="warm")
+        sine_bias = keep.tile([P, 1], F32, name="sine_bias")
 
         nc.vector.memset(mix_s_raw[:].bitcast(I32), 0)
         nc.vector.memset(tab_s[:].bitcast(I32), 0)
         nc.vector.memset(zero[:], 0.0)
-        nc.scalar.activation(out=warm[:], in_=zero[:], func=ACT.Sin)
+        nc.scalar.activation(out=sine_bias[:], in_=zero[:], func=ACT.Sin)
         nc.vector.memset(wq_s[:].bitcast(I32), 0)
         for page in pages:
             nc.vector.memset(page[:], 0.0)
 
-        def load_raw(rows, name):
-            raw = ring.tile([P, PACK, KP], F32, name=name, tag="raw", bufs=5)
+        def load_rows(rows, name):
+            raw = ring.tile([P, PACK, KP], F32, name=name, tag="raw", bufs=RAW_BUFS)
             nc.sync.dma_start(out=raw[:], in_=rows.rearrange("(p j) c -> p j c", j=PACK))
             return raw
 
-        def quantize(raw, order, copies, name, tag="grouped", bufs=4):
-            grouped = ring.tile([P, PACK * KP], BF16, name=name + "_g", tag=tag, bufs=bufs, align_bytes=64)
-            dst = grouped[:].rearrange(order + " -> p m j t", t=PACK, j=PACK)
-            src = raw[:].rearrange("p j (m t) -> p m j t", t=PACK)
-            share = P // len(copies)
-            for u, copy in enumerate(copies):
-                copy(out=dst[:, u * share : (u + 1) * share], in_=src[:, u * share : (u + 1) * share])
-            codes = keep.tile([P, KP], U32, name=name + "_c", align_bytes=64)
-            scales = keep.tile([P, KP], U8, name=name + "_s", align_bytes=64)
-            nc.vector.quantize_mx(out=codes[:].bitcast(FP8X4), scales=scales[:], in_=grouped[:])
-            return codes, scales
-
-        phase_sb = keep.tile([P, HB, PACK], F32, name="phase_sb")
-        amp_sb = keep.tile([P, HB, PACK], F32, name="amp_sb")
-        base_sb = keep.tile([P, NC], F32, name="base_sb")
+        def load_planes(planes, scales):
+            for e in range(4):
+                nc.sync.dma_start(
+                    out=planes[e:P:QUADRANT, :].bitcast(I32).rearrange("q (a c) -> q a c", a=H_PASSES),
+                    in_=scales[:, e:16:4, :].bitcast(I32).rearrange("a q c -> q a c"),
+                )
 
         x_raw = {}
         tab_w = []
+        cap_sb = {}
 
         def load_x(b, a):
-            x_raw[b, a] = load_raw(x[a * KP : (a + 1) * KP, b * KP : (b + 1) * KP], f"x_raw{b}{a}")
+            x_raw[b, a] = load_rows(x[a * KP : (a + 1) * KP, b * KP : (b + 1) * KP], f"x_raw{b}{a}")
 
         def load_table(a):
             words = keep.tile([P, T], I32, name=f"tab_w{a}")
             nc.sync.dma_start(out=words[:], in_=tab_words[a].rearrange("p t i -> p (t i)").bitcast(I32))
             tab_w.append(words)
 
+        def load_cap(n):
+            b, i = divmod(n, PACK)
+            rows = cap[b * KP : (b + 1) * KP, :].rearrange("(p i) t -> p i t", i=PACK)
+            pair = keep.tile([P, 2, T2], F32, name=f"cap{n}")
+            nc.sync.dma_start(out=pair[:], in_=rows[:, i : i + 2, :])
+            cap_sb[n] = pair[:, 0, :]
+            cap_sb[n + 1] = pair[:, 1, :]
+
+        phase_sb = keep.tile([P, H_PASSES, PACK], F32, name="phase_sb")
+        amp_sb = keep.tile([P, H_PASSES, PACK], F32, name="amp_sb")
+        base_sb = keep.tile([P, N // P], F32, name="base_sb")
+        mix_w_raw = keep.tile([P, H_PASSES * H // 2], I32, name="mix_w_raw")
+        wgs_sb = keep.tile([P, S], F32, name="wgs_sb")
+        wq_w = keep.tile([P, H_PASSES * N], I32, name="wq_w", align_bytes=64)
+
         nc.sync.dma_start(offs_sb[:], offs)
-        nc.sync.dma_start(out=phase_sb[:], in_=phase.rearrange("(b p i) -> p b i", b=HB, i=PACK))
-        mix_w_raw = keep.tile([P, HB * H // 2], I32, name="mix_w_raw")
+        nc.sync.dma_start(out=phase_sb[:], in_=phase.rearrange("(b p i) -> p b i", b=H_PASSES, i=PACK))
         nc.sync.dma_start(
-            out=mix_w_raw[:].rearrange("p (a c) -> p a c", a=HB),
+            out=mix_w_raw[:].rearrange("p (a c) -> p a c", a=H_PASSES),
             in_=mix_words.bitcast(I32).rearrange("a p c -> p a c"),
         )
-        xs_raw = [load_raw(xs[0:KP, :], "xs_raw0")]
-        for q in range(4):
-            nc.sync.dma_start(
-                out=mix_s_raw[32 * q : 32 * q + 4, :].bitcast(I32).rearrange("r (a c) -> r a c", a=HB),
-                in_=mix_scales[:, 4 * q : 4 * q + 4, :].bitcast(I32).rearrange("a r c -> r a c"),
-            )
-        xs_raw.append(load_raw(xs[KP : 2 * KP, :], "xs_raw1"))
+        xs_raw = [load_rows(xs[0:KP, :], "xs_raw0")]
+        load_planes(mix_s_raw, mix_scales)
+        xs_raw.append(load_rows(xs[KP : 2 * KP, :], "xs_raw1"))
         load_x(0, 0)
         load_table(0)
-        for q in range(4):
+        for quad in range(P // QUADRANT):
             nc.sync.dma_start(
-                out=tab_s[32 * q : 32 * q + 4 * KA, :].bitcast(I32),
-                in_=tab_scales[:, 4 * q : 4 * q + 4, :].bitcast(I32),
+                out=tab_s[QUADRANT * quad : QUADRANT * quad + 4 * K_PASSES, :].bitcast(I32),
+                in_=tab_scales[:, 4 * quad : 4 * quad + 4, :].bitcast(I32),
             )
-        load_x(0, 1)
-        load_table(1)
-        load_x(0, 2)
-        load_table(2)
+        for a in range(1, K_PASSES):
+            load_x(0, a)
+            load_table(a)
         nc.sync.dma_start(offs2_sb[:], offs2)
-        wgs_sb = keep.tile([P, S], F32, name="wgs_sb")
         nc.sync.dma_start(out=wgs_sb[:], in_=wgs)
-        nc.sync.dma_start(out=amp_sb[:], in_=amp.rearrange("(b p i) -> p b i", b=HB, i=PACK))
-
-        cap_sb = {}
-
-        def load_cap(b, u):
-            rows = cap[b * KP : (b + 1) * KP, :].rearrange("(p i) t -> p i t", i=PACK)
-            pair = keep.tile([P, 2, T2], F32, name=f"cap{b}{u}")
-            nc.sync.dma_start(out=pair[:], in_=rows[:, 2 * u : 2 * u + 2, :])
-            cap_sb[b, 2 * u] = pair[:, 0, :]
-            cap_sb[b, 2 * u + 1] = pair[:, 1, :]
-
-        load_cap(0, 0)
-        for a in range(KA):
+        nc.sync.dma_start(out=amp_sb[:], in_=amp.rearrange("(b p i) -> p b i", b=H_PASSES, i=PACK))
+        load_x(1, 0)
+        load_cap(0)
+        for a in range(1, K_PASSES):
             load_x(1, a)
-        load_cap(0, 1)
-        for u in range(2):
-            load_cap(1, u)
-        wq_w = keep.tile([P, HB * N], I32, name="wq_w", align_bytes=64)
+        for n in range(2, SLICES, 2):
+            load_cap(n)
         nc.sync.dma_start(
-            out=wq_w[:].rearrange("p (a c) -> p a c", a=HB),
+            out=wq_w[:].rearrange("p (a c) -> p a c", a=H_PASSES),
             in_=wq_words.rearrange("a p c i -> p a (c i)").bitcast(I32),
         )
-        for q in range(4):
-            nc.sync.dma_start(
-                out=wq_s[32 * q : 32 * q + 4, :].bitcast(I32).rearrange("r (a c) -> r a c", a=HB),
-                in_=wq_scales[:, 4 * q : 4 * q + 4, :].bitcast(I32).rearrange("a r c -> r a c"),
-            )
-
-        with nc.allow_non_contiguous_dma(reason="one bias value to a partition"):
+        load_planes(wq_s, wq_scales)
+        with nc.allow_non_contiguous_dma(reason="one value of base to a partition"):
             nc.sync.dma_start(out=base_sb[:], in_=base.rearrange("(c p) -> p c", p=P))
 
-        shift = keep.tile([P, HB * PACK], F32, name="shift")
+        def quantize_rows(raw, order, copies, name, tag="grouped", bufs=4):
+            grouped = ring.tile([P, PACK * KP], BF16, name=name + "_g", tag=tag, bufs=bufs, align_bytes=64)
+            dst = grouped[:].rearrange(order + " -> p m j t", t=PACK, j=PACK)
+            src = raw[:].rearrange("p j (m t) -> p m j t", t=PACK)
+            share = PACK // len(copies)
+            for u, copy in enumerate(copies):
+                copy(out=dst[:, :, :, u * share : (u + 1) * share], in_=src[:, :, :, u * share : (u + 1) * share])
+            codes = keep.tile([P, KP], U32, name=name + "_c", align_bytes=64)
+            scales = keep.tile([P, KP], U8, name=name + "_s", align_bytes=64)
+            nc.vector.quantize_mx(out=codes[:].bitcast(FP8X4), scales=scales[:], in_=grouped[:])
+            return codes, scales
+
+        as_they_lie = "p (m t j)"
+        by_slice = "p (t m j)"
+
+        shift = keep.tile([P, SLICES], F32, name="shift")
         nc.vector.tensor_scalar(
             out=shift[:], in0=phase_sb[:].rearrange("p b i -> p (b i)"),
             scalar1=1.0 / TURN, scalar2=-0.25, op0=ALU.mult, op1=ALU.add,
         )
-        mix_w = keep.tile([P, HB * H * 2], U8, name="mix_w", align_bytes=64)
+        mix_w = keep.tile([P, H_PASSES * H * 2], U8, name="mix_w", align_bytes=64)
         nc.vector.tensor_copy(
             out=mix_w[:].bitcast(U16).rearrange("p (g t m) -> p g t m", t=PACK, m=P),
             in_=mix_w_raw[:].bitcast(U16).rearrange("p (g m t) -> p g t m", t=PACK, m=P),
         )
-        mix_s = keep.tile([P, HB * H], U8, name="mix_s", align_bytes=64)
+        mix_s = keep.tile([P, H_PASSES * H], U8, name="mix_s", align_bytes=64)
         nc.vector.tensor_copy(
             out=mix_s[:].rearrange("p (g t m) -> p g t m", t=PACK, m=P),
             in_=mix_s_raw[:].rearrange("p (g m t) -> p g t m", t=PACK, m=P),
         )
-        xs_q = [quantize(xs_raw[a], "p (m t j)", [nc.vector.tensor_copy], f"xs{a}") for a in range(HB)]
-        x_q = {}
+        xs_q = [quantize_rows(xs_raw[a], as_they_lie, [nc.vector.tensor_copy], f"xs{a}") for a in range(H_PASSES)]
 
-        v_w = [keep.tile([P, S], U32, name=f"v_w{a}", align_bytes=64) for a in range(KA)]
+        v_w = [keep.tile([P, S], U32, name=f"v_w{a}", align_bytes=64) for a in range(K_PASSES)]
+        v_s = keep.tile([P, S], U8, name="v_s", align_bytes=64)
 
-        def gather_words(a, c0, c1):
+        def gather_words(a, j0, j1):
             nc.vector.tensor_copy(
-                v_w[a][:, c0:c1], tab_w[a][:].bitcast(U32).indirect(offs_sb[:, c0 // 16 : c1 // 16])
+                v_w[a][:, j0:j1], tab_w[a][:].bitcast(U32).indirect(offs_sb[:, j0 // GROUP : j1 // GROUP])
             )
 
-        x_q[0, 0] = quantize(x_raw[0, 0], "p (t m j)", [nc.scalar.copy], "x00")
+        x_q = {}
+        x_q[0, 0] = quantize_rows(x_raw[0, 0], by_slice, [nc.scalar.copy], "x00")
         gather_words(0, 0, S)
-        v_s = keep.tile([P, S], U8, name="v_s", align_bytes=64)
         nc.vector.tensor_copy(v_s[:], tab_s[:].indirect(offs_sb[:]))
-        x_q[0, 1] = quantize(x_raw[0, 1], "p (t m j)", [nc.scalar.copy], "x01")
+        x_q[0, 1] = quantize_rows(x_raw[0, 1], by_slice, [nc.scalar.copy], "x01")
         gather_words(1, 0, S)
-        x_q[0, 2] = quantize(x_raw[0, 2], "p (t m j)", [nc.scalar.copy, nc.vector.tensor_copy], "x02")
+        x_q[0, 2] = quantize_rows(x_raw[0, 2], by_slice, [nc.scalar.copy, nc.vector.tensor_copy], "x02")
         gather_words(2, 0, HALF)
         gather_words(2, HALF, S)
 
-        def mix_pass(acc, n, a, c0, c1, start):
-            b, i = divmod(n, PACK)
-            col = a * H + b * KP + i * P
-            step = S if c1 - c0 == S else P
-            for c in range(c0, c1, step):
-                nc.tensor.matmul_mx(
-                    out=acc[:, c - c0 : c - c0 + step],
-                    lhsT=mix_w[:, 2 * col : 2 * (col + P)].bitcast(FP4X4),
-                    lhsT_scale=mix_s[:, col : col + P],
-                    rhs=xs_q[a][0][:, c : c + step].bitcast(FP8X4), rhs_scale=xs_q[a][1][:, c : c + step],
-                    start=(start and c == c0), stop=False,
-                )
-
-        def table_pass(acc, n, a, c0, c1):
-            b, i = divmod(n, PACK)
-            codes, scales = x_q[b, a]
-            nc.tensor.matmul_mx(
-                out=acc[:],
-                lhsT=codes[:, i * P : (i + 1) * P].bitcast(FP8X4),
-                lhsT_scale=scales[:, i * P : (i + 1) * P],
-                rhs=v_w[a][:, c0:c1].bitcast(FP8X4), rhs_scale=v_s[4 * a : P, c0:c1],
-                start=False, stop=(a == KA - 1),
-            )
-
-        def first_product(parts, first_bank):
-            accs = [
-                psum.tile([P, c1 - c0], F32, name=f"acc{n}_{c0}", tag=f"bank{(first_bank + u) % 8}")
-                for u, (n, c0, c1) in enumerate(parts)
+        def open_sums(parts, first_bank):
+            sums = [
+                psum.tile([P, j1 - j0], F32, name=f"a{n}_{j0}", tag=f"bank{(first_bank + u) % BANKS}")
+                for u, (n, j0, j1) in enumerate(parts)
             ]
-            for a in range(HB):
-                for acc, (n, c0, c1) in zip(accs, parts):
-                    mix_pass(acc, n, a, c0, c1, a == 0)
-            return accs
+            for a in range(H_PASSES):
+                codes, scales = xs_q[a]
+                for acc, (n, j0, j1) in zip(sums, parts):
+                    col = a * H + n * P
+                    width = S if j1 - j0 == S else P
+                    for j in range(j0, j1, width):
+                        nc.tensor.matmul_mx(
+                            out=acc[:, j - j0 : j - j0 + width],
+                            lhsT=mix_w[:, 2 * col : 2 * (col + P)].bitcast(FP4X4),
+                            lhsT_scale=mix_s[:, col : col + P],
+                            rhs=codes[:, j : j + width].bitcast(FP8X4), rhs_scale=scales[:, j : j + width],
+                            start=(a == 0 and j == j0), stop=False,
+                        )
+            return sums
 
-        def finish_product(accs, parts):
-            for a in range(KA):
-                for acc, (n, c0, c1) in zip(accs, parts):
-                    table_pass(acc, n, a, c0, c1)
+        def table_passes(sums, parts, passes):
+            for a in passes:
+                for acc, (n, j0, j1) in zip(sums, parts):
+                    b, i = divmod(n, PACK)
+                    codes, scales = x_q[b, a]
+                    nc.tensor.matmul_mx(
+                        out=acc[:],
+                        lhsT=codes[:, i * P : (i + 1) * P].bitcast(FP8X4),
+                        lhsT_scale=scales[:, i * P : (i + 1) * P],
+                        rhs=v_w[a][:, j0:j1].bitcast(FP8X4), rhs_scale=v_s[4 * a : P, j0:j1],
+                        start=False, stop=(a == K_PASSES - 1),
+                    )
 
-        def sine_tile(n, width, name):
-            if n == 3:
-                return ring.tile([P, width], F32, name=name, tag="held", bufs=1, align_bytes=64)
-            return ring.tile([P, width], F32, name=name, tag="s", bufs=3)
-
-        def fold(acc, n, c0, c1):
-            w = ring.tile([P, c1 - c0], F32, name=f"w{n}_{c0}", tag="w", bufs=4)
+        def sine(acc, n, j0=0, j1=S):
+            width = j1 - j0
+            w = ring.tile([P, width], F32, name=f"w{n}_{j0}", tag="w", bufs=4)
             nc.scalar.activation(out=w[:], in_=acc[:], func=ACT.Abs, bias=shift[:, n : n + 1], scale=1.0 / TURN)
-            k = ring.tile([P, c1 - c0], U32, name=f"k{n}_{c0}", tag="k", bufs=3)
+            k = ring.tile([P, width], U32, name=f"k{n}_{j0}", tag="k", bufs=3)
             if n == 0:
                 nc.vector.tensor_scalar(
                     out=k[:].bitcast(I32), in0=w[:], scalar1=-0.25, scalar2=None, op0=ALU.add
                 )
             else:
                 nc.scalar.activation(out=k[:], in_=w[:], func=ACT.Copy, bias=-0.25, scale=1.0)
-            return w, k
-
-        def sine(acc, n, c0=0, c1=S):
-            w, k = fold(acc, n, c0, c1)
-            m = ring.tile([P, c1 - c0], F32, name=f"m{n}_{c0}", tag="m", bufs=2)
+            turns = ring.tile([P, width], F32, name=f"turns{n}_{j0}", tag="turns", bufs=2)
             nc.vector.scalar_tensor_tensor(
-                out=m[:], in0=k[:].bitcast(I32), scalar=0.25, in1=w[:], op0=ALU.add, op1=ALU.subtract,
+                out=turns[:], in0=k[:].bitcast(I32), scalar=0.25, in1=w[:], op0=ALU.add, op1=ALU.subtract,
             )
-            s = sine_tile(n, c1 - c0, f"s{n}_{c0}")
-            nc.scalar.activation(out=s[:], in_=m[:], func=ACT.Sin, scale=TURN)
+            if n == HELD_SLICE:
+                s = ring.tile([P, width], F32, name=f"s{n}_{j0}", tag="held", bufs=1, align_bytes=64)
+            else:
+                s = ring.tile([P, width], F32, name=f"s{n}_{j0}", tag="s", bufs=3)
+            nc.scalar.activation(out=s[:], in_=turns[:], func=ACT.Sin, bias=sine_bias[:], scale=TURN)
             return s
 
-        def scatter(s, n, c0=0, c1=S):
+        def scatter(s, n, j0=0, j1=S):
             nc.vector.tensor_tensor(
-                pages[n % PAGES][:].indirect(offs2_sb[:, c0 // 16 : c1 // 16]), s[:], wgs_sb[:, c0:c1], ALU.mult
+                pages[n % PAGES][:].indirect(offs2_sb[:, j0 // GROUP : j1 // GROUP]),
+                s[:], wgs_sb[:, j0:j1], ALU.mult,
             )
 
-        z_rows = [keep.tile([P, PACK * T2], BF16, name=f"z_rows{b}") for b in range(HB)]
+        z_rows = [keep.tile([P, PACK * T2], BF16, name=f"z_rows{b}") for b in range(H_PASSES)]
 
-        def capped(n, c0, c1):
+        def capped(n, t0=0, t1=T2):
             b, i = divmod(n, PACK)
             nc.vector.scalar_tensor_tensor(
-                out=z_rows[b][:, i * T2 + c0 : i * T2 + c1], in0=pages[n % PAGES][:, c0:c1],
-                scalar=amp_sb[:, b, i : i + 1], in1=cap_sb[b, i][:, c0:c1], op0=ALU.mult, op1=ALU.min,
+                out=z_rows[b][:, i * T2 + t0 : i * T2 + t1], in0=pages[n % PAGES][:, t0:t1],
+                scalar=amp_sb[:, b, i : i + 1], in1=cap_sb[n][:, t0:t1], op0=ALU.mult, op1=ALU.min,
             )
 
-        z_c = [keep.tile([P, T2], U32, name=f"z_c{b}", align_bytes=64) for b in range(HB)]
-        z_s = [keep.tile([P, T2], U8, name=f"z_s{b}", align_bytes=64) for b in range(HB)]
+        z_c = [keep.tile([P, T2], U32, name=f"z_c{b}", align_bytes=64) for b in range(H_PASSES)]
+        z_s = [keep.tile([P, T2], U8, name=f"z_s{b}", align_bytes=64) for b in range(H_PASSES)]
 
-        def weave(b, c0, c1, copy):
-            woven = ring.tile([P, (c1 - c0) * PACK], BF16, name=f"woven{b}_{c0}", tag="grouped", bufs=4, align_bytes=64)
+        def weave(b, t0, t1, copy):
+            woven = ring.tile([P, (t1 - t0) * PACK], BF16, name=f"woven{b}_{t0}", tag="grouped", bufs=4, align_bytes=64)
+            rows = z_rows[b][:].rearrange("p (i c) -> p i c", i=PACK)[:, :, t0:t1]
             copy(
                 out=woven[:].rearrange("p (m t i) -> p m i t", t=PACK, i=PACK),
-                in_=z_rows[b][:].rearrange("p (i c) -> p i c", i=PACK)[:, :, c0:c1].rearrange(
-                    "p i (m t) -> p m i t", t=PACK
-                ),
+                in_=rows.rearrange("p i (m t) -> p m i t", t=PACK),
             )
             return woven
 
-        def quantize_z(b, c0, c1, woven):
-            nc.vector.quantize_mx(out=z_c[b][:, c0:c1].bitcast(FP8X4), scales=z_s[b][:, c0:c1], in_=woven[:])
+        def quantize_z(b, t0, t1, woven):
+            nc.vector.quantize_mx(out=z_c[b][:, t0:t1].bitcast(FP8X4), scales=z_s[b][:, t0:t1], in_=woven[:])
+
+        def chunk(q):
+            return q * CHUNK, (q + 1) * CHUNK
 
         def second_pass(b, q):
-            cols = slice(q * CH, (q + 1) * CH)
+            cols = slice(*chunk(q))
             for h in range(2):
                 for e in range(2):
                     col = b * N + (2 * h + e) * P
                     nc.tensor.matmul_mx(
-                        out=banks[q][h][:, e * CH : (e + 1) * CH],
+                        out=y[q][h][:, e * CHUNK : (e + 1) * CHUNK],
                         lhsT=wq_w[:, col : col + P].bitcast(FP8X4), lhsT_scale=wq_s[:, col : col + P],
                         rhs=z_c[b][:, cols].bitcast(FP8X4), rhs_scale=z_s[b][:, cols],
-                        start=(b == 0 and e == 0), stop=(b == HB - 1 and e == 1),
+                        start=(b == 0 and e == 0), stop=(b == H_PASSES - 1 and e == 1),
                     )
-
-        late = sine
-        parts0 = [(0, 0, HALF), (0, HALF, S), (1, 0, S), (2, 0, S), (3, 0, S)]
-        parts1 = [(n, 0, S) for n in range(PACK, 2 * PACK)]
-        accs0 = first_product(parts0, 7)
-        for acc, part in zip(accs0, parts0):
-            table_pass(acc, part[0], 0, part[1], part[2])
-        for lo, hi in ((0, 2), (2, 5)):
-            for a in range(1, KA):
-                for acc, part in zip(accs0[lo:hi], parts0[lo:hi]):
-                    table_pass(acc, part[0], a, part[1], part[2])
-        first_a = sine(accs0[0], 0, 0, HALF)
-        first_b = sine(accs0[1], 0, HALF, S)
-        scatter(first_a, 0, 0, HALF)
-        sines = {1: sine(accs0[2], 1)}
-        scatter(first_b, 0, HALF, S)
-        sines[2] = sine(accs0[3], 2)
-        accs1 = first_product(parts1, 4)
-        scatter(sines[1], 1)
-        capped(0, 0, T2)
-        for a in range(KA - 1):
-            x_q[1, a] = quantize(x_raw[1, a], "p (t m j)", [nc.scalar.copy], f"x1{a}")
-        x_q[1, 2] = quantize(x_raw[1, 2], "p (t m j)", [nc.scalar.copy], "x12", "held", 1)
-        finish_product(accs1, parts1)
-        sines[3] = late(accs0[4], 3)
-        scatter(sines[2], 2)
-        capped(1, 0, T2)
-        sines[4] = sine(accs1[0], 4)
-        scatter(sines[3], 3)
-        capped(2, 0, T2)
-        sines[5] = late(accs1[1], 5)
-        scatter(sines[4], 4)
-        capped(3, 0, T2)
-        sines[6] = late(accs1[2], 6)
-        scatter(sines[5], 5)
-        capped(4, 0, T2)
-        sines[7] = late(accs1[3], 7)
-        banks = [
-            [psum.tile([P, 2 * CH], F32, name=f"y{q}{h}", tag=f"bank{(4 + 2 * q + h) % 8}") for h in range(2)]
-            for q in range(NCH)
-        ]
-        woven0 = [weave(0, u * 2 * CH, (u + 1) * 2 * CH, nc.scalar.copy) for u in range(2)]
-        scatter(sines[6], 6)
-        capped(5, 0, T2)
-        for u in range(2):
-            quantize_z(0, u * 2 * CH, (u + 1) * 2 * CH, woven0[u])
-        for q in range(NCH):
-            second_pass(0, q)
-        capped(6, 0, T2)
-        scatter(sines[7], 7)
-
-        stage = [ring.tile([P, 8 * CH], F32, name=f"stage{u}", tag="raw", bufs=5) for u in range(2)]
 
         def emit(q):
             for h in range(2):
-                at = (2 * (q % 2) + h) * 2 * CH
-                staged = stage[q // 2][:, at : at + 2 * CH]
-                if q >= NCH - 2 and h == 0:
+                at = (2 * (q % 2) + h) * 2 * CHUNK
+                staged = stage[q // 2][:, at : at + 2 * CHUNK]
+                if q >= CHUNKS - VECTOR_CHUNKS and h == 0:
                     nc.vector.tensor_tensor(
                         staged.rearrange("p (e t) -> p e t", e=2),
-                        banks[q][h][:].rearrange("p (e t) -> p e t", e=2),
-                        base_sb[:, 2 * h : 2 * h + 2].unsqueeze(2).to_broadcast([P, 2, CH]),
+                        y[q][h][:].rearrange("p (e t) -> p e t", e=2),
+                        base_sb[:, 2 * h : 2 * h + 2].unsqueeze(2).to_broadcast([P, 2, CHUNK]),
                         ALU.add,
                     )
                 else:
                     for e in range(2):
-                        c = 2 * h + e
                         nc.scalar.activation(
-                            out=staged[:, e * CH : (e + 1) * CH], in_=banks[q][h][:, e * CH : (e + 1) * CH],
-                            func=ACT.Identity, bias=base_sb[:, c : c + 1], scale=1.0,
+                            out=staged[:, e * CHUNK : (e + 1) * CHUNK], in_=y[q][h][:, e * CHUNK : (e + 1) * CHUNK],
+                            func=ACT.Identity, bias=base_sb[:, 2 * h + e : 2 * h + e + 1], scale=1.0,
                         )
                 nc.sync.dma_start(
-                    out=out[2 * h * P : (2 * h + 2) * P, q * CH : (q + 1) * CH].rearrange("(e p) t -> p e t", p=P),
+                    out=out[2 * h * P : (2 * h + 2) * P, slice(*chunk(q))].rearrange("(e p) t -> p e t", p=P),
                     in_=staged.rearrange("p (e t) -> p e t", e=2),
                 )
 
-        def chunk(q):
-            return q * CH, (q + 1) * CH
+        parts0 = [(0, 0, HALF), (0, HALF, S)] + [(n, 0, S) for n in range(1, PACK)]
+        parts1 = [(n, 0, S) for n in range(PACK, SLICES)]
+        sums0 = open_sums(parts0, BANKS - 1)
+        table_passes(sums0, parts0, [0])
+        table_passes(sums0[:2], parts0[:2], range(1, K_PASSES))
+        table_passes(sums0[2:], parts0[2:], range(1, K_PASSES))
+        halves = [sine(acc, *part) for acc, part in zip(sums0[:2], parts0[:2])]
+        scatter(halves[0], *parts0[0])
+        sines = {1: sine(sums0[2], 1)}
+        scatter(halves[1], *parts0[1])
+        sines[2] = sine(sums0[3], 2)
+        sums1 = open_sums(parts1, PACK)
+        scatter(sines[1], 1)
+        capped(0)
 
-        capped(7, *chunk(0))
-        capped(7, *chunk(1))
+        for a in range(K_PASSES - 1):
+            x_q[1, a] = quantize_rows(x_raw[1, a], by_slice, [nc.scalar.copy], f"x1{a}")
+        x_q[1, K_PASSES - 1] = quantize_rows(x_raw[1, K_PASSES - 1], by_slice, [nc.scalar.copy], "x12", "held", 1)
+        table_passes(sums1[:1], parts1[:1], range(K_PASSES))
+        table_passes(sums1[1:], parts1[1:], range(K_PASSES))
+        sums = {3: sums0[4], 4: sums1[0], 5: sums1[1], 6: sums1[2], 7: sums1[3]}
+
+        sines[3] = sine(sums[3], 3)
+        for n in range(2, LAST - 1):
+            scatter(sines[n], n)
+            capped(n - 1)
+            sines[n + 2] = sine(sums[n + 2], n + 2)
+
+        y = [
+            [psum.tile([P, 2 * CHUNK], F32, name=f"y{q}{h}", tag=f"bank{(PACK + 2 * q + h) % BANKS}") for h in range(2)]
+            for q in range(CHUNKS)
+        ]
+        halves_of_page = [(0, T2 // 2), (T2 // 2, T2)]
+        woven0 = [weave(0, t0, t1, nc.scalar.copy) for t0, t1 in halves_of_page]
+        scatter(sines[LAST - 1], LAST - 1)
+        capped(LAST - 2)
+        for (t0, t1), woven in zip(halves_of_page, woven0):
+            quantize_z(0, t0, t1, woven)
+        for q in range(CHUNKS):
+            second_pass(0, q)
+        capped(LAST - 1)
+        scatter(sines[LAST], LAST)
+
+        stage = [ring.tile([P, 8 * CHUNK], F32, name=f"stage{u}", tag="raw", bufs=RAW_BUFS) for u in range(CHUNKS // 2)]
+        capped(LAST, *chunk(0))
+        capped(LAST, *chunk(1))
         woven1 = {1: weave(1, *chunk(1), nc.scalar.copy)}
         woven1[0] = weave(1, *chunk(0), nc.vector.tensor_copy)
-        capped(7, *chunk(2))
-        quantize_z(1, *chunk(0), woven1[0])
-        second_pass(1, 0)
-        emit(0)
-        capped(7, *chunk(3))
-        quantize_z(1, *chunk(1), woven1[1])
-        second_pass(1, 1)
-        emit(1)
-        woven1[2] = weave(1, *chunk(2), nc.vector.tensor_copy)
-        woven1[3] = weave(1, *chunk(3), nc.vector.tensor_copy)
-        for q in range(2, NCH):
+        for q in range(2):
+            capped(LAST, *chunk(q + 2))
             quantize_z(1, *chunk(q), woven1[q])
             second_pass(1, q)
-        for q in range(2, NCH):
+            emit(q)
+        for q in range(2, CHUNKS):
+            woven1[q] = weave(1, *chunk(q), nc.vector.tensor_copy)
+        for q in range(2, CHUNKS):
+            quantize_z(1, *chunk(q), woven1[q])
+            second_pass(1, q)
+        for q in range(2, CHUNKS):
             emit(q)

@@ -2,6 +2,7 @@ import math
 from contextlib import ExitStack
 
 import concourse.mybir as mybir
+from concourse.masks import make_identity
 
 K, H, N, T, S, T2 = 1536, 1024, 512, 2048, 512, 1024
 FLOPS = 2 * K * H * S + 2 * H * H * S + 2 * H * N * T2
@@ -33,7 +34,9 @@ CHUNKS = T2 // CHUNK
 VECTOR_CHUNKS = 2
 PAGES = 3
 RAW_BUFS = 5
+SINE_BUFS = 4
 HELD_SLICE = 3
+TURNED_FROM = 6
 TURN = 2.0 * math.pi
 
 
@@ -222,6 +225,26 @@ def tile_list_tariff_lane_smoothing_kernel(
                         start=False, stop=(a == K_PASSES - 1),
                     )
 
+        ident = keep.tile([P, P], F32, name="ident")
+        make_identity(nc, ident[:])
+
+        def sine_turned(w, k, n):
+            minus_k = ring.tile([P, S], F32, name=f"minus_k{n}", tag="turns", bufs=2)
+            nc.scalar.activation(out=minus_k[:], in_=k[:], func=ACT.Copy, bias=-0.25, scale=-1.0)
+            blocks = [slice(u * P, (u + 1) * P) for u in range(S // P)]
+            angle = psum.tile([P, S], F32, name=f"angle{n}", tag=f"bank{2 * (n % 2)}")
+            for cols in blocks:
+                nc.tensor.matmul(angle[:, cols], w[:, cols], ident[:], start=True, stop=False, is_transpose=True)
+                nc.tensor.matmul(angle[:, cols], minus_k[:, cols], ident[:], start=False, stop=True, is_transpose=True)
+            turned = ring.tile([P, S], F32, name=f"turned{n}", tag="turned", bufs=2)
+            nc.scalar.activation(out=turned[:], in_=angle[:], func=ACT.Sin, bias=sine_bias[:], scale=-TURN)
+            back = psum.tile([P, S], F32, name=f"back{n}", tag=f"bank{2 * (n % 2) + 1}")
+            for cols in blocks:
+                nc.tensor.transpose(back[:, cols], turned[:, cols], ident[:])
+            s = ring.tile([P, S], F32, name=f"s{n}", tag="s", bufs=SINE_BUFS)
+            nc.scalar.copy(out=s[:], in_=back[:])
+            return s
+
         def sine(acc, n, j0=0, j1=S):
             width = j1 - j0
             w = ring.tile([P, width], F32, name=f"w{n}_{j0}", tag="w", bufs=4)
@@ -233,6 +256,8 @@ def tile_list_tariff_lane_smoothing_kernel(
                 )
             else:
                 nc.scalar.activation(out=k[:], in_=w[:], func=ACT.Copy, bias=-0.25, scale=1.0)
+            if n >= TURNED_FROM:
+                return sine_turned(w, k, n)
             turns = ring.tile([P, width], F32, name=f"turns{n}_{j0}", tag="turns", bufs=2)
             nc.vector.scalar_tensor_tensor(
                 out=turns[:], in0=k[:].bitcast(I32), scalar=0.25, in1=w[:], op0=ALU.add, op1=ALU.subtract,
@@ -240,7 +265,7 @@ def tile_list_tariff_lane_smoothing_kernel(
             if n == HELD_SLICE:
                 s = ring.tile([P, width], F32, name=f"s{n}_{j0}", tag="held", bufs=1, align_bytes=64)
             else:
-                s = ring.tile([P, width], F32, name=f"s{n}_{j0}", tag="s", bufs=3)
+                s = ring.tile([P, width], F32, name=f"s{n}_{j0}", tag="s", bufs=SINE_BUFS)
             nc.scalar.activation(out=s[:], in_=turns[:], func=ACT.Sin, bias=sine_bias[:], scale=TURN)
             return s
 

@@ -29,13 +29,14 @@ GROUP = 16
 QUADRANT = 32
 BANKS = 8
 HALF = S // 2
+HALF_PAGE = T2 // 2
 CHUNK = 256
 CHUNKS = T2 // CHUNK
 VECTOR_CHUNKS = 2
 PAGES = 3
 RAW_BUFS = 5
 SINE_BUFS = 4
-HELD_SLICE = 3
+HELD_SLICES = (3, LAST)
 TURNED_FROM = 6
 TURN = 2.0 * math.pi
 
@@ -228,6 +229,11 @@ def tile_list_tariff_lane_smoothing_kernel(
         ident = keep.tile([P, P], F32, name="ident")
         make_identity(nc, ident[:])
 
+        def sine_tile(n, j0, width):
+            if n in HELD_SLICES:
+                return ring.tile([P, width], F32, name=f"s{n}_{j0}", tag="held", bufs=1, align_bytes=64)
+            return ring.tile([P, width], F32, name=f"s{n}_{j0}", tag="s", bufs=SINE_BUFS)
+
         def sine_turned(w, k, n):
             minus_k = ring.tile([P, S], F32, name=f"minus_k{n}", tag="turns", bufs=2)
             nc.scalar.activation(out=minus_k[:], in_=k[:], func=ACT.Copy, bias=-0.25, scale=-1.0)
@@ -241,7 +247,7 @@ def tile_list_tariff_lane_smoothing_kernel(
             back = psum.tile([P, S], F32, name=f"back{n}", tag=f"bank{2 * (n % 2) + 1}")
             for cols in blocks:
                 nc.tensor.transpose(back[:, cols], turned[:, cols], ident[:])
-            s = ring.tile([P, S], F32, name=f"s{n}", tag="s", bufs=SINE_BUFS)
+            s = sine_tile(n, 0, S)
             nc.scalar.copy(out=s[:], in_=back[:])
             return s
 
@@ -262,10 +268,7 @@ def tile_list_tariff_lane_smoothing_kernel(
             nc.vector.scalar_tensor_tensor(
                 out=turns[:], in0=k[:].bitcast(I32), scalar=0.25, in1=w[:], op0=ALU.add, op1=ALU.subtract,
             )
-            if n == HELD_SLICE:
-                s = ring.tile([P, width], F32, name=f"s{n}_{j0}", tag="held", bufs=1, align_bytes=64)
-            else:
-                s = ring.tile([P, width], F32, name=f"s{n}_{j0}", tag="s", bufs=SINE_BUFS)
+            s = sine_tile(n, j0, width)
             nc.scalar.activation(out=s[:], in_=turns[:], func=ACT.Sin, bias=sine_bias[:], scale=TURN)
             return s
 
@@ -284,7 +287,7 @@ def tile_list_tariff_lane_smoothing_kernel(
                 scalar=amp_sb[:, b, i : i + 1], in1=cap_sb[n][:, t0:t1], op0=ALU.mult, op1=ALU.min,
             )
 
-        z_c = [keep.tile([P, T2], U32, name=f"z_c{b}", align_bytes=64) for b in range(H_PASSES)]
+        z_c = {(b, u): keep.tile([P, HALF_PAGE], U32, name=f"z_c{b}{u}", align_bytes=64) for b, u in ((0, 0), (1, 0), (1, 1))}
         z_s = [keep.tile([P, T2], U8, name=f"z_s{b}", align_bytes=64) for b in range(H_PASSES)]
 
         def weave(b, t0, t1, copy):
@@ -296,8 +299,12 @@ def tile_list_tariff_lane_smoothing_kernel(
             )
             return woven
 
+        def z_words(b, t0, t1):
+            u, at = divmod(t0, HALF_PAGE)
+            return z_c[b, u][:, at : at + t1 - t0].bitcast(FP8X4)
+
         def quantize_z(b, t0, t1, woven):
-            nc.vector.quantize_mx(out=z_c[b][:, t0:t1].bitcast(FP8X4), scales=z_s[b][:, t0:t1], in_=woven[:])
+            nc.vector.quantize_mx(out=z_words(b, t0, t1), scales=z_s[b][:, t0:t1], in_=woven[:])
 
         def chunk(q):
             return q * CHUNK, (q + 1) * CHUNK
@@ -310,7 +317,7 @@ def tile_list_tariff_lane_smoothing_kernel(
                     nc.tensor.matmul_mx(
                         out=y[q][h][:, e * CHUNK : (e + 1) * CHUNK],
                         lhsT=wq_w[:, col : col + P].bitcast(FP8X4), lhsT_scale=wq_s[:, col : col + P],
-                        rhs=z_c[b][:, cols].bitcast(FP8X4), rhs_scale=z_s[b][:, cols],
+                        rhs=z_words(b, *chunk(q)), rhs_scale=z_s[b][:, cols],
                         start=(b == 0 and e == 0), stop=(b == H_PASSES - 1 and e == 1),
                     )
 
@@ -368,16 +375,19 @@ def tile_list_tariff_lane_smoothing_kernel(
             [psum.tile([P, 2 * CHUNK], F32, name=f"y{q}{h}", tag=f"bank{(PACK + 2 * q + h) % BANKS}") for h in range(2)]
             for q in range(CHUNKS)
         ]
-        halves_of_page = [(0, T2 // 2), (T2 // 2, T2)]
-        woven0 = [weave(0, t0, t1, nc.scalar.copy) for t0, t1 in halves_of_page]
+        woven0 = [weave(0, u * HALF_PAGE, (u + 1) * HALF_PAGE, nc.scalar.copy) for u in range(2)]
         scatter(sines[LAST - 1], LAST - 1)
         capped(LAST - 2)
-        for (t0, t1), woven in zip(halves_of_page, woven0):
-            quantize_z(0, t0, t1, woven)
-        for q in range(CHUNKS):
+        quantize_z(0, 0, HALF_PAGE, woven0[0])
+        for q in range(CHUNKS // 2):
             second_pass(0, q)
         capped(LAST - 1)
         scatter(sines[LAST], LAST)
+
+        z_c[0, 1] = ring.tile([P, HALF_PAGE], U32, name="z_c01", tag="held", bufs=1, align_bytes=64)
+        quantize_z(0, HALF_PAGE, T2, woven0[1])
+        for q in range(CHUNKS // 2, CHUNKS):
+            second_pass(0, q)
 
         stage = [ring.tile([P, 8 * CHUNK], F32, name=f"stage{u}", tag="raw", bufs=RAW_BUFS) for u in range(CHUNKS // 2)]
         capped(LAST, *chunk(0))

import math
from contextlib import ExitStack

import concourse.mybir as mybir
from concourse.masks import make_identity

K, H, N, T, S, T2 = 1536, 1024, 512, 2048, 512, 1024
FLOPS = 2 * K * H * S + 2 * H * H * S + 2 * H * N * T2

F32 = mybir.dt.float32
BF16 = mybir.dt.bfloat16
I32 = mybir.dt.int32
U32 = mybir.dt.uint32
U16 = mybir.dt.uint16
U8 = mybir.dt.uint8
FP8X4 = mybir.dt.float8_e4m3fn_x4
FP4X4 = mybir.dt.float4_e2m1fn_x4
ALU = mybir.AluOpType
ACT = mybir.ActivationFunctionType

P = 128
PACK = 4
KP = P * PACK
K_PASSES = K // KP
H_PASSES = H // KP
SLICES = H_PASSES * PACK
LAST = SLICES - 1
GROUP = 16
QUADRANT = 32
BANKS = 8
HALF = S // 2
HALF_PAGE = T2 // 2
CHUNK = 256
CHUNKS = T2 // CHUNK
VECTOR_CHUNKS = 2
PAGES = 3
RAW_BUFS = 5
SINE_BUFS = 4
HELD_SLICES = (3, LAST)
TURNED_FROM = 6
TURN = 2.0 * math.pi


def tile_list_tariff_lane_smoothing_kernel(
    tc, tab_words, tab_scales, offs, x, xs, mix_words, mix_scales, phase, amp,
    wgs, offs2, cap, wq_words, wq_scales, base, out,
):
    nc = tc.nc
    with ExitStack() as ctx:
        keep = ctx.enter_context(tc.tile_pool(name="keep", bufs=1))
        ring = ctx.enter_context(tc.tile_pool(name="ring", bufs=2))
        psum = ctx.enter_context(tc.psum_pool(name="psum", bufs=1))

        offs_sb = keep.tile([P, S // GROUP], U16, name="offs_sb")
        offs2_sb = keep.tile([P, S // GROUP], U16, name="offs2_sb")
        tab_s = keep.tile([P, T], U8, name="tab_s", align_bytes=64)
        mix_s_raw = keep.tile([P, H_PASSES * H], U8, name="mix_s_raw", align_bytes=64)
        wq_s = keep.tile([P, H_PASSES * N], U8, name="wq_s", align_bytes=64)
        pages = [keep.tile([P, T2], F32, name=f"page{u}") for u in range(PAGES)]
        zero = keep.tile([P, 1], F32, name="zero")
        sine_bias = keep.tile([P, 1], F32, name="sine_bias")

        nc.vector.memset(mix_s_raw[:].bitcast(I32), 0)
        nc.vector.memset(tab_s[:].bitcast(I32), 0)
        nc.vector.memset(zero[:], 0.0)
        nc.scalar.activation(out=sine_bias[:], in_=zero[:], func=ACT.Sin)
        nc.vector.memset(wq_s[:].bitcast(I32), 0)
        for page in pages:
            nc.vector.memset(page[:], 0.0)

        def load_rows(rows, name):
            raw = ring.tile([P, PACK, KP], F32, name=name, tag="raw", bufs=RAW_BUFS)
            nc.sync.dma_start(out=raw[:], in_=rows.rearrange("(p j) c -> p j c", j=PACK))
            return raw

        def load_planes(planes, scales):
            for e in range(4):
                nc.sync.dma_start(
                    out=planes[e:P:QUADRANT, :].bitcast(I32).rearrange("q (a c) -> q a c", a=H_PASSES),
                    in_=scales[:, e:16:4, :].bitcast(I32).rearrange("a q c -> q a c"),
                )

        x_raw = {}
        tab_w = []
        cap_sb = {}

        def load_x(b, a):
            x_raw[b, a] = load_rows(x[a * KP : (a + 1) * KP, b * KP : (b + 1) * KP], f"x_raw{b}{a}")

        def load_table(a):
            words = keep.tile([P, T], I32, name=f"tab_w{a}")
            nc.sync.dma_start(out=words[:], in_=tab_words[a].rearrange("p t i -> p (t i)").bitcast(I32))
            tab_w.append(words)

        def load_cap(n):
            b, i = divmod(n, PACK)
            rows = cap[b * KP : (b + 1) * KP, :].rearrange("(p i) t -> p i t", i=PACK)
            pair = keep.tile([P, 2, T2], F32, name=f"cap{n}")
            nc.sync.dma_start(out=pair[:], in_=rows[:, i : i + 2, :])
            cap_sb[n] = pair[:, 0, :]
            cap_sb[n + 1] = pair[:, 1, :]

        phase_sb = keep.tile([P, H_PASSES, PACK], F32, name="phase_sb")
        amp_sb = keep.tile([P, H_PASSES, PACK], F32, name="amp_sb")
        base_sb = keep.tile([P, N // P], F32, name="base_sb")
        mix_w_raw = keep.tile([P, H_PASSES * H // 2], I32, name="mix_w_raw")
        wgs_sb = keep.tile([P, S], F32, name="wgs_sb")
        wq_w = keep.tile([P, H_PASSES * N], I32, name="wq_w", align_bytes=64)

        nc.sync.dma_start(offs_sb[:], offs)
        nc.sync.dma_start(out=phase_sb[:], in_=phase.rearrange("(b p i) -> p b i", b=H_PASSES, i=PACK))
        nc.sync.dma_start(
            out=mix_w_raw[:].rearrange("p (a c) -> p a c", a=H_PASSES),
            in_=mix_words.bitcast(I32).rearrange("a p c -> p a c"),
        )
        xs_raw = [load_rows(xs[0:KP, :], "xs_raw0")]
        load_planes(mix_s_raw, mix_scales)
        xs_raw.append(load_rows(xs[KP : 2 * KP, :], "xs_raw1"))
        load_x(0, 0)
        load_table(0)
        for quad in range(P // QUADRANT):
            nc.sync.dma_start(
                out=tab_s[QUADRANT * quad : QUADRANT * quad + 4 * K_PASSES, :].bitcast(I32),
                in_=tab_scales[:, 4 * quad : 4 * quad + 4, :].bitcast(I32),
            )
        for a in range(1, K_PASSES):
            load_x(0, a)
            load_table(a)
        nc.sync.dma_start(offs2_sb[:], offs2)
        nc.sync.dma_start(out=wgs_sb[:], in_=wgs)
        nc.sync.dma_start(out=amp_sb[:], in_=amp.rearrange("(b p i) -> p b i", b=H_PASSES, i=PACK))
        load_x(1, 0)
        load_cap(0)
        for a in range(1, K_PASSES):
            load_x(1, a)
        for n in range(2, SLICES, 2):
            load_cap(n)
        nc.sync.dma_start(
            out=wq_w[:].rearrange("p (a c) -> p a c", a=H_PASSES),
            in_=wq_words.rearrange("a p c i -> p a (c i)").bitcast(I32),
        )
        load_planes(wq_s, wq_scales)
        with nc.allow_non_contiguous_dma(reason="one value of base to a partition"):
            nc.sync.dma_start(out=base_sb[:], in_=base.rearrange("(c p) -> p c", p=P))

        def quantize_rows(raw, order, copies, name, tag="grouped", bufs=4):
            grouped = ring.tile([P, PACK * KP], BF16, name=name + "_g", tag=tag, bufs=bufs, align_bytes=64)
            dst = grouped[:].rearrange(order + " -> p m j t", t=PACK, j=PACK)
            src = raw[:].rearrange("p j (m t) -> p m j t", t=PACK)
            share = PACK // len(copies)
            for u, copy in enumerate(copies):
                copy(out=dst[:, :, :, u * share : (u + 1) * share], in_=src[:, :, :, u * share : (u + 1) * share])
            codes = keep.tile([P, KP], U32, name=name + "_c", align_bytes=64)
            scales = keep.tile([P, KP], U8, name=name + "_s", align_bytes=64)
            nc.vector.quantize_mx(out=codes[:].bitcast(FP8X4), scales=scales[:], in_=grouped[:])
            return codes, scales

        as_they_lie = "p (m t j)"
        by_slice = "p (t m j)"

        shift = keep.tile([P, SLICES], F32, name="shift")
        nc.vector.tensor_scalar(
            out=shift[:], in0=phase_sb[:].rearrange("p b i -> p (b i)"),
            scalar1=1.0 / TURN, scalar2=-0.25, op0=ALU.mult, op1=ALU.add,
        )
        mix_w = keep.tile([P, H_PASSES * H * 2], U8, name="mix_w", align_bytes=64)
        nc.vector.tensor_copy(
            out=mix_w[:].bitcast(U16).rearrange("p (g t m) -> p g t m", t=PACK, m=P),
            in_=mix_w_raw[:].bitcast(U16).rearrange("p (g m t) -> p g t m", t=PACK, m=P),
        )
        mix_s = keep.tile([P, H_PASSES * H], U8, name="mix_s", align_bytes=64)
        nc.vector.tensor_copy(
            out=mix_s[:].rearrange("p (g t m) -> p g t m", t=PACK, m=P),
            in_=mix_s_raw[:].rearrange("p (g m t) -> p g t m", t=PACK, m=P),
        )
        xs_q = [quantize_rows(xs_raw[a], as_they_lie, [nc.vector.tensor_copy], f"xs{a}") for a in range(H_PASSES)]

        v_w = [keep.tile([P, S], U32, name=f"v_w{a}", align_bytes=64) for a in range(K_PASSES)]
        v_s = keep.tile([P, S], U8, name="v_s", align_bytes=64)

        def gather_words(a, j0, j1):
            nc.vector.tensor_copy(
                v_w[a][:, j0:j1], tab_w[a][:].bitcast(U32).indirect(offs_sb[:, j0 // GROUP : j1 // GROUP])
            )

        x_q = {}
        x_q[0, 0] = quantize_rows(x_raw[0, 0], by_slice, [nc.scalar.copy], "x00")
        gather_words(0, 0, S)
        nc.vector.tensor_copy(v_s[:], tab_s[:].indirect(offs_sb[:]))
        x_q[0, 1] = quantize_rows(x_raw[0, 1], by_slice, [nc.scalar.copy], "x01")
        gather_words(1, 0, S)
        x_q[0, 2] = quantize_rows(x_raw[0, 2], by_slice, [nc.scalar.copy, nc.vector.tensor_copy], "x02")
        gather_words(2, 0, HALF)
        gather_words(2, HALF, S)

        def open_sums(parts, first_bank):
            sums = [
                psum.tile([P, j1 - j0], F32, name=f"a{n}_{j0}", tag=f"bank{(first_bank + u) % BANKS}")
                for u, (n, j0, j1) in enumerate(parts)
            ]
            for a in range(H_PASSES):
                codes, scales = xs_q[a]
                for acc, (n, j0, j1) in zip(sums, parts):
                    col = a * H + n * P
                    width = S if j1 - j0 == S else P
                    for j in range(j0, j1, width):
                        nc.tensor.matmul_mx(
                            out=acc[:, j - j0 : j - j0 + width],
                            lhsT=mix_w[:, 2 * col : 2 * (col + P)].bitcast(FP4X4),
                            lhsT_scale=mix_s[:, col : col + P],
                            rhs=codes[:, j : j + width].bitcast(FP8X4), rhs_scale=scales[:, j : j + width],
                            start=(a == 0 and j == j0), stop=False,
                        )
            return sums

        def table_passes(sums, parts, passes):
            for a in passes:
                for acc, (n, j0, j1) in zip(sums, parts):
                    b, i = divmod(n, PACK)
                    codes, scales = x_q[b, a]
                    nc.tensor.matmul_mx(
                        out=acc[:],
                        lhsT=codes[:, i * P : (i + 1) * P].bitcast(FP8X4),
                        lhsT_scale=scales[:, i * P : (i + 1) * P],
                        rhs=v_w[a][:, j0:j1].bitcast(FP8X4), rhs_scale=v_s[4 * a : P, j0:j1],
                        start=False, stop=(a == K_PASSES - 1),
                    )

        ident = keep.tile([P, P], F32, name="ident")
        make_identity(nc, ident[:])

        def sine_tile(n, j0, width):
            if n in HELD_SLICES:
                return ring.tile([P, width], F32, name=f"s{n}_{j0}", tag="held", bufs=1, align_bytes=64)
            return ring.tile([P, width], F32, name=f"s{n}_{j0}", tag="s", bufs=SINE_BUFS)

        def sine_turned(w, k, n):
            minus_k = ring.tile([P, S], F32, name=f"minus_k{n}", tag="turns", bufs=2)
            nc.scalar.activation(out=minus_k[:], in_=k[:], func=ACT.Copy, bias=-0.25, scale=-1.0)
            blocks = [slice(u * P, (u + 1) * P) for u in range(S // P)]
            angle = psum.tile([P, S], F32, name=f"angle{n}", tag=f"bank{2 * (n % 2)}")
            for cols in blocks:
                nc.tensor.matmul(angle[:, cols], w[:, cols], ident[:], start=True, stop=False, is_transpose=True)
                nc.tensor.matmul(angle[:, cols], minus_k[:, cols], ident[:], start=False, stop=True, is_transpose=True)
            turned = ring.tile([P, S], F32, name=f"turned{n}", tag="turned", bufs=2)
            nc.scalar.activation(out=turned[:], in_=angle[:], func=ACT.Sin, bias=sine_bias[:], scale=-TURN)
            back = psum.tile([P, S], F32, name=f"back{n}", tag=f"bank{2 * (n % 2) + 1}")
            for cols in blocks:
                nc.tensor.transpose(back[:, cols], turned[:, cols], ident[:])
            s = sine_tile(n, 0, S)
            nc.scalar.copy(out=s[:], in_=back[:])
            return s

        def sine(acc, n, j0=0, j1=S):
            width = j1 - j0
            w = ring.tile([P, width], F32, name=f"w{n}_{j0}", tag="w", bufs=4)
            nc.scalar.activation(out=w[:], in_=acc[:], func=ACT.Abs, bias=shift[:, n : n + 1], scale=1.0 / TURN)
            k = ring.tile([P, width], U32, name=f"k{n}_{j0}", tag="k", bufs=3)
            if n == 0:
                nc.vector.tensor_scalar(
                    out=k[:].bitcast(I32), in0=w[:], scalar1=-0.25, scalar2=None, op0=ALU.add
                )
            else:
                nc.scalar.activation(out=k[:], in_=w[:], func=ACT.Copy, bias=-0.25, scale=1.0)
            if n >= TURNED_FROM:
                return sine_turned(w, k, n)
            turns = ring.tile([P, width], F32, name=f"turns{n}_{j0}", tag="turns", bufs=2)
            nc.vector.scalar_tensor_tensor(
                out=turns[:], in0=k[:].bitcast(I32), scalar=0.25, in1=w[:], op0=ALU.add, op1=ALU.subtract,
            )
            s = sine_tile(n, j0, width)
            nc.scalar.activation(out=s[:], in_=turns[:], func=ACT.Sin, bias=sine_bias[:], scale=TURN)
            return s

        def scatter(s, n, j0=0, j1=S):
            nc.vector.tensor_tensor(
                pages[n % PAGES][:].indirect(offs2_sb[:, j0 // GROUP : j1 // GROUP]),
                s[:], wgs_sb[:, j0:j1], ALU.mult,
            )

        z_rows = [keep.tile([P, PACK * T2], BF16, name=f"z_rows{b}") for b in range(H_PASSES)]

        def capped(n, t0=0, t1=T2):
            b, i = divmod(n, PACK)
            nc.vector.scalar_tensor_tensor(
                out=z_rows[b][:, i * T2 + t0 : i * T2 + t1], in0=pages[n % PAGES][:, t0:t1],
                scalar=amp_sb[:, b, i : i + 1], in1=cap_sb[n][:, t0:t1], op0=ALU.mult, op1=ALU.min,
            )

        z_c = {(b, u): keep.tile([P, HALF_PAGE], U32, name=f"z_c{b}{u}", align_bytes=64) for b, u in ((0, 0), (1, 0), (1, 1))}
        z_s = [keep.tile([P, T2], U8, name=f"z_s{b}", align_bytes=64) for b in range(H_PASSES)]

        def weave(b, t0, t1, copy):
            woven = ring.tile([P, (t1 - t0) * PACK], BF16, name=f"woven{b}_{t0}", tag="grouped", bufs=4, align_bytes=64)
            rows = z_rows[b][:].rearrange("p (i c) -> p i c", i=PACK)[:, :, t0:t1]
            copy(
                out=woven[:].rearrange("p (m t i) -> p m i t", t=PACK, i=PACK),
                in_=rows.rearrange("p i (m t) -> p m i t", t=PACK),
            )
            return woven

        def z_words(b, t0, t1):
            u, at = divmod(t0, HALF_PAGE)
            return z_c[b, u][:, at : at + t1 - t0].bitcast(FP8X4)

        def quantize_z(b, t0, t1, woven):
            nc.vector.quantize_mx(out=z_words(b, t0, t1), scales=z_s[b][:, t0:t1], in_=woven[:])

        def chunk(q):
            return q * CHUNK, (q + 1) * CHUNK

        def second_pass(b, q):
            cols = slice(*chunk(q))
            for h in range(2):
                for e in range(2):
                    col = b * N + (2 * h + e) * P
                    nc.tensor.matmul_mx(
                        out=y[q][h][:, e * CHUNK : (e + 1) * CHUNK],
                        lhsT=wq_w[:, col : col + P].bitcast(FP8X4), lhsT_scale=wq_s[:, col : col + P],
                        rhs=z_words(b, *chunk(q)), rhs_scale=z_s[b][:, cols],
                        start=(b == 0 and e == 0), stop=(b == H_PASSES - 1 and e == 1),
                    )

        def emit(q):
            for h in range(2):
                at = (2 * (q % 2) + h) * 2 * CHUNK
                staged = stage[q // 2][:, at : at + 2 * CHUNK]
                if q >= CHUNKS - VECTOR_CHUNKS and h == 0:
                    nc.vector.tensor_tensor(
                        staged.rearrange("p (e t) -> p e t", e=2),
                        y[q][h][:].rearrange("p (e t) -> p e t", e=2),
                        base_sb[:, 2 * h : 2 * h + 2].unsqueeze(2).to_broadcast([P, 2, CHUNK]),
                        ALU.add,
                    )
                else:
                    for e in range(2):
                        nc.scalar.activation(
                            out=staged[:, e * CHUNK : (e + 1) * CHUNK], in_=y[q][h][:, e * CHUNK : (e + 1) * CHUNK],
                            func=ACT.Identity, bias=base_sb[:, 2 * h + e : 2 * h + e + 1], scale=1.0,
                        )
                nc.sync.dma_start(
                    out=out[2 * h * P : (2 * h + 2) * P, slice(*chunk(q))].rearrange("(e p) t -> p e t", p=P),
                    in_=staged.rearrange("p (e t) -> p e t", e=2),
                )

        parts0 = [(0, 0, HALF), (0, HALF, S)] + [(n, 0, S) for n in range(1, PACK)]
        parts1 = [(n, 0, S) for n in range(PACK, SLICES)]
        sums0 = open_sums(parts0, BANKS - 1)
        table_passes(sums0, parts0, [0])
        table_passes(sums0[:2], parts0[:2], range(1, K_PASSES))
        table_passes(sums0[2:], parts0[2:], range(1, K_PASSES))
        halves = [sine(acc, *part) for acc, part in zip(sums0[:2], parts0[:2])]
        scatter(halves[0], *parts0[0])
        sines = {1: sine(sums0[2], 1)}
        scatter(halves[1], *parts0[1])
        sines[2] = sine(sums0[3], 2)
        sums1 = open_sums(parts1, PACK)
        scatter(sines[1], 1)
        capped(0)

        for a in range(K_PASSES - 1):
            x_q[1, a] = quantize_rows(x_raw[1, a], by_slice, [nc.scalar.copy], f"x1{a}")
        x_q[1, K_PASSES - 1] = quantize_rows(x_raw[1, K_PASSES - 1], by_slice, [nc.scalar.copy], "x12", "held", 1)
        table_passes(sums1[:1], parts1[:1], range(K_PASSES))
        table_passes(sums1[1:], parts1[1:], range(K_PASSES))
        sums = {3: sums0[4], 4: sums1[0], 5: sums1[1], 6: sums1[2], 7: sums1[3]}

        sines[3] = sine(sums[3], 3)
        for n in range(2, LAST - 1):
            scatter(sines[n], n)
            capped(n - 1)
            sines[n + 2] = sine(sums[n + 2], n + 2)

        y = [
            [psum.tile([P, 2 * CHUNK], F32, name=f"y{q}{h}", tag=f"bank{(PACK + 2 * q + h) % BANKS}") for h in range(2)]
            for q in range(CHUNKS)
        ]
        woven0 = [weave(0, u * HALF_PAGE, (u + 1) * HALF_PAGE, nc.scalar.copy) for u in range(2)]
        scatter(sines[LAST - 1], LAST - 1)
        capped(LAST - 2)
        quantize_z(0, 0, HALF_PAGE, woven0[0])
        for q in range(CHUNKS // 2):
            second_pass(0, q)
        capped(LAST - 1)
        scatter(sines[LAST], LAST)

        z_c[0, 1] = ring.tile([P, HALF_PAGE], U32, name="z_c01", tag="held", bufs=1, align_bytes=64)
        quantize_z(0, HALF_PAGE, T2, woven0[1])
        for q in range(CHUNKS // 2, CHUNKS):
            second_pass(0, q)

        stage = [ring.tile([P, 8 * CHUNK], F32, name=f"stage{u}", tag="raw", bufs=RAW_BUFS) for u in range(CHUNKS // 2)]
        capped(LAST, *chunk(0))
        capped(LAST, *chunk(1))
        woven1 = {1: weave(1, *chunk(1), nc.scalar.copy)}
        woven1[0] = weave(1, *chunk(0), nc.vector.tensor_copy)
        for q in range(2):
            capped(LAST, *chunk(q + 2))
            quantize_z(1, *chunk(q), woven1[q])
            second_pass(1, q)
            emit(q)
        for q in range(2, CHUNKS):
            woven1[q] = weave(1, *chunk(q), nc.vector.tensor_copy)
        for q in range(2, CHUNKS):
            quantize_z(1, *chunk(q), woven1[q])
            second_pass(1, q)
        for q in range(2, CHUNKS):
            emit(q)
